import numpy as np
import ml_dtypes


def mxq(x, axis, fmt="e4m3"):
    dtype, down = {"e4m3": (ml_dtypes.float8_e4m3fn, 7), "e5m2": (ml_dtypes.float8_e5m2, 14)}[fmt]
    v = np.moveaxis(np.asarray(x, np.float32).astype(ml_dtypes.bfloat16).astype(np.float64), axis, -1)
    blocks = v.reshape(v.shape[:-1] + (-1, 32))
    amax = np.abs(blocks).max(-1, keepdims=True)
    byte = np.maximum(np.where(amax > 0, np.frexp(amax)[1] - 1 + 127, 0) - down, 1)
    scale = np.exp2(byte - 127.0)
    codes = (blocks / scale).astype(np.float32).astype(dtype).astype(np.float64)
    return np.moveaxis((codes * scale).reshape(v.shape), -1, axis)


WIDE = False


def mx_kscale(k):
    if not WIDE:
        return np.ones(k)
    levels = np.array([10, -10, 5, -5, 0])
    if k % 512:
        return np.exp2(np.random.permutation(np.resize(levels, k // 32))).repeat(32)
    a = np.empty((k // 512, 16))
    for p in range(k // 512):
        a[p, :8] = np.random.permutation(np.resize(levels, 8))
        for g in range(8):
            far = levels[np.abs(levels - a[p, g]) >= 10]
            a[p, g + 8] = far[np.random.randint(len(far))]
    return np.exp2(a.ravel()).repeat(32)


def f64(x):
    return np.asarray(x).astype(np.float64)


def striped(idx):
    return np.tile(idx.reshape(-1, 16).T, (8, 1)).astype(np.uint16)


def unstriped(offs):
    return offs[:16].T.reshape(-1).astype(np.int64)


def striped8(idx):
    return np.concatenate([x.reshape(-1, 16).T for x in idx]).astype(np.uint16)


def runs(offs, k):
    lists = np.stack([offs[16 * r : 16 * r + 16].T.reshape(-1) for r in range(8)]).astype(np.int64)
    return lists[np.arange(k) % 512 // 64]


def pack_weight(w):
    k, n = w.shape
    w = f64(np.asarray(w, np.float32).astype(ml_dtypes.bfloat16)).reshape(k // 32, 32, n)
    amax = np.abs(w).max(1)
    byte = np.clip(np.where(amax > 0, np.frexp(amax)[1] - 1 + 127 - 7, 1), 1, 254)
    scaled = (w * np.exp2(127.0 - byte)[:, None, :]).reshape(k, n).astype(np.float32)
    words = np.ascontiguousarray(scaled.reshape(k // 512, 128, 4, n).transpose(0, 1, 3, 2)).astype(ml_dtypes.float8_e4m3fn).view(np.uint8)
    return words, np.ascontiguousarray(byte.astype(np.uint8).reshape(k // 512, 16, n))


def unpack_weight(words, scales):
    g, p, n, _ = words.shape
    vals = np.ascontiguousarray(words).view(ml_dtypes.float8_e4m3fn).astype(np.float64) * np.repeat(np.exp2(scales.astype(np.float64) - 127.0), 8, axis=1)[..., None]
    return vals.transpose(0, 1, 3, 2).reshape(g * 512, n)


def relu(v):
    return np.maximum(v, 0.0)


K, T, S, H, N, V = 1024, 2048, 1024, 512, 128, 512


def setup_inputs():
    n = np.random.standard_normal
    s = mx_kscale(K)[:, None]
    u = mx_kscale(H)
    packed_xT = pack_weight(n((K, T)) * s)
    packed_w2 = pack_weight(n((H, N)) / np.sqrt(H) / u[:, None])
    return {
        "x_words": packed_xT[0],
        "x_scales": packed_xT[1],
        "w1": (n((K, H)) / np.sqrt(K) / s * u).astype(np.float32),
        "w2_words": packed_w2[0],
        "w2_scales": packed_w2[1],
        "offs": striped8(np.stack([np.random.permutation(T)[:S] for _ in range(8)])),
        "left": striped(np.random.permutation(S)[:V]),
        "right": striped(np.random.permutation(S)[:V]),
    }


def reference(x_words, x_scales, w1, w2_words, w2_scales, offs, left, right):
    xq = unpack_weight(x_words, x_scales)[np.arange(K)[:, None], runs(offs, K)]
    h = mxq(f64(w1), 0, "e4m3").T @ xq
    z = relu(h[:, unstriped(left)] - h[:, unstriped(right)])
    return unpack_weight(w2_words, w2_scales).T @ mxq(z, 0, "e4m3")

@@ -1,0 +1,207 @@
+from contextlib import ExitStack
+
+import concourse.mybir as mybir
+
+K, T, S, H, N, V = 1024, 2048, 1024, 512, 128, 512
+FLOPS = 2 * K * H * S + 2 * H * N * V
+
+F32 = mybir.dt.float32
+BF16 = mybir.dt.bfloat16
+I32 = mybir.dt.int32
+U32 = mybir.dt.uint32
+U16 = mybir.dt.uint16
+U8 = mybir.dt.uint8
+FP8X4 = mybir.dt.float8_e4m3fn_x4
+ALU = mybir.AluOpType
+ACT = mybir.ActivationFunctionType
+
+P = 128
+PACK = 4
+K_PASS = P * PACK
+PASSES = K // K_PASS
+BANK = 512
+PER_COLUMN = 16
+PAIR_CHUNKS = ((0, 256), (256, 384), (384, 512))
+
+
+def tile_picked_phpair_relu_p_kernel(tc, x_words, x_scales, w1, w2_words, w2_scales, offs, left, right, out):
+    nc = tc.nc
+    with ExitStack() as ctx:
+        lists = ctx.enter_context(tc.tile_pool(name="lists", bufs=1))
+        keep = ctx.enter_context(tc.tile_pool(name="keep", bufs=1))
+        shared = ctx.enter_context(tc.tile_pool(name="shared", bufs=1))
+        psum = ctx.enter_context(tc.psum_pool(name="psum", bufs=1))
+
+        offs_sb = lists.tile([P, S // PER_COLUMN], U16, name="offs_sb")
+        left_sb = lists.tile([P, V // PER_COLUMN], U16, name="left_sb")
+        right_sb = lists.tile([P, V // PER_COLUMN], U16, name="right_sb")
+        nc.sync.dma_start(offs_sb[:], offs)
+
+        scale_table = shared.tile([P, T], U8, name="scale_table", align_bytes=64, offset=4 * T - T // 2)
+        nc.gpsimd.memset(scale_table[:].bitcast(I32), 0)
+        rows = x_scales.bitcast(I32).rearrange("z (r j) c -> j r z c", j=2)
+        for j in range(2):
+            nc.scalar.dma_start(scale_table[j:P:8, :].bitcast(I32), rows[j])
+
+        word_table = [
+            keep.tile([P, T], I32, name="word_table0", align_bytes=64),
+            shared.tile([P, T], I32, name="word_table1", align_bytes=64, offset=0),
+        ]
+        w_first = keep.tile([P, PACK, H], F32, name="w_first")
+        w_halves = shared.tile([P, 2, PACK, H // 2], F32, name="w_halves", align_bytes=64, offset=4 * T)
+        w_second = [w_halves[:, u, :, :] for u in range(2)]
+        w1_rows = w1.rearrange("(z p t) c -> z p t c", z=PASSES, t=PACK)
+
+        def load_words(z):
+            nc.sync.dma_start(word_table[z][:], x_words[z].rearrange("p n t -> p (n t)").bitcast(I32))
+
+        load_words(0)
+        nc.sync.dma_start(left_sb[:], left)
+        nc.sync.dma_start(right_sb[:], right)
+        nc.sync.dma_start(w_first[:], w1_rows[0])
+
+        w2_codes = keep.tile([P, N], I32, name="w2_codes", align_bytes=64)
+        w2_plane = keep.tile([P, N], U8, name="w2_plane", align_bytes=64)
+        nc.gpsimd.memset(w2_plane[:], 0)
+        nc.gpsimd.dma_start(w2_codes[:], w2_words[0].rearrange("p n t -> p (n t)").bitcast(I32))
+        for q in range(4):
+            nc.gpsimd.dma_start(w2_plane[32 * q : 32 * q + 4, :].bitcast(I32), w2_scales[0].bitcast(I32)[4 * q : 4 * q + 4, :])
+
+        picked_scales = keep.tile([P, S], U8, name="picked_scales", align_bytes=64)
+        x_plane = keep.tile([P, S], U8, name="x_plane", align_bytes=64)
+        nc.vector.tensor_copy(picked_scales[:], scale_table[:].indirect(offs_sb[:]))
+        load_words(1)
+        for u in range(2):
+            nc.sync.dma_start(w_second[u], w1_rows[1][:, :, u * (H // 2) : (u + 1) * (H // 2)])
+        nc.vector.tensor_copy(x_plane[:].bitcast(I32), picked_scales[:].bitcast(I32))
+        for z in range(PASSES):
+            for j in range(2):
+                nc.scalar.dma_start(
+                    x_plane[8 * z + 2 + j : P : 32, :].bitcast(I32),
+                    picked_scales[16 + 8 * z + j : P : 32, :].bitcast(I32),
+                )
+
+        x_codes = [keep.tile([P, S], U32, name=f"x_codes{z}", align_bytes=64) for z in range(PASSES)]
+
+        def pick_words(z):
+            nc.vector.tensor_copy(x_codes[z][:], word_table[z][:].bitcast(U32).indirect(offs_sb[:]))
+
+        w_bf16 = [[keep.tile([P, 2, P, PACK], BF16, name=f"w_bf16_{z}{d}", align_bytes=64) for d in range(2)] for z in range(PASSES)]
+        w_codes = [[keep.tile([P, 2 * P], U32, name=f"w_codes{z}{d}", align_bytes=64) for d in range(2)] for z in range(PASSES)]
+        w_plane = [[keep.tile([P, 2 * P], U8, name=f"w_plane{z}{d}", align_bytes=64) for d in range(2)] for z in range(PASSES)]
+
+        def deal_views(z, d, raw, m0, m1):
+            dst = w_bf16[z][d][:, :, m0:m1, :].rearrange("p s m t -> p m s t")
+            src = raw.rearrange("p t (m s) -> p m s t", s=PACK)[:, :, 2 * d : 2 * d + 2, :]
+            return dst, src
+
+        def deal_on_scalar(z, d, raw, m0, m1):
+            dst, src = deal_views(z, d, raw, m0, m1)
+            nc.scalar.copy(dst, src)
+
+        def deal_on_vector(z, d, raw, m0, m1):
+            dst, src = deal_views(z, d, raw, m0, m1)
+            nc.vector.tensor_copy(dst, src)
+
+        def quantize_w(z, d, s0, s1):
+            nc.vector.quantize_mx(
+                out=w_codes[z][d][:, s0 * P : s1 * P].bitcast(FP8X4),
+                scales=w_plane[z][d][:, s0 * P : s1 * P],
+                in_=w_bf16[z][d][:, s0:s1, :, :].rearrange("p s m t -> p (s m t)"),
+            )
+
+        banks = [[psum.tile([P, BANK], F32, name=f"bank{s}{u}") for u in range(2)] for s in range(PACK)]
+
+        def first_layer_pass(z, s):
+            d, cols = s // 2, slice((s % 2) * P, (s % 2 + 1) * P)
+            for u in range(2):
+                places = slice(u * BANK, (u + 1) * BANK)
+                nc.tensor.matmul_mx(
+                    out=banks[s][u][:],
+                    lhsT=w_codes[z][d][:, cols].bitcast(FP8X4),
+                    lhsT_scale=w_plane[z][d][:, cols],
+                    rhs=x_codes[z][:, places].bitcast(FP8X4),
+                    rhs_scale=x_plane[8 * z : P, places],
+                    start=(z == 0),
+                    stop=(z == PASSES - 1),
+                )
+
+        pick_words(0)
+        for d in range(2):
+            deal_on_scalar(0, d, w_first[:], 0, P)
+        quantize_w(0, 0, 0, 2)
+        pick_words(1)
+        for d in range(2):
+            deal_on_scalar(1, d, w_second[0], 0, P // 2)
+        deal_on_vector(1, 0, w_second[1], P // 2, P)
+        deal_on_scalar(1, 1, w_second[1], P // 2, P)
+        quantize_w(1, 0, 0, 1)
+        quantize_w(1, 0, 1, 2)
+        quantize_w(0, 1, 0, 2)
+        quantize_w(1, 1, 0, 2)
+        for s in range(2):
+            first_layer_pass(0, s)
+        for s in range(2):
+            first_layer_pass(1, s)
+        for s in range(2, PACK):
+            for z in range(PASSES):
+                first_layer_pass(z, s)
+
+        h = [keep.tile([P, S], F32, name=f"h{s}") for s in range(PACK)]
+        nc.scalar.copy(h[0][:, :BANK], banks[0][0][:])
+        nc.vector.tensor_copy(h[0][:, BANK:], banks[0][1][:])
+        for s in range(1, PACK):
+            for u in range(2):
+                nc.scalar.copy(h[s][:, u * BANK : (u + 1) * BANK], banks[s][u][:])
+
+        def entries(index, c):
+            v0, v1 = PAIR_CHUNKS[c]
+            return index[:, v0 // PER_COLUMN : v1 // PER_COLUMN]
+
+        h_right = [[None] * len(PAIR_CHUNKS) for s in range(PACK)]
+
+        def fetch_right(s):
+            for c, (v0, v1) in enumerate(PAIR_CHUNKS):
+                tag = f"handed_on{c}" if s == PACK - 1 else f"h_right{s}{c}"
+                h_right[s][c] = keep.tile([P, v1 - v0], F32, name=f"h_right{s}{c}", tag=tag)
+                nc.vector.tensor_copy(h_right[s][c][:], h[s][:].indirect(entries(right_sb, c)))
+
+        def subtract(diff, s, c):
+            nc.vector.tensor_tensor(diff[:, s, :], h[s][:].indirect(entries(left_sb, c)), h_right[s][c][:], ALU.subtract)
+
+        def second_layer(diff, c):
+            v0, v1 = PAIR_CHUNKS[c]
+            n = v1 - v0
+            z_bf16 = keep.tile([P, n, PACK], BF16, name=f"z_bf16_{c}", align_bytes=64)
+            if c == len(PAIR_CHUNKS) - 1:
+                nc.vector.tensor_scalar(z_bf16[:], diff[:].rearrange("p s v -> p v s"), 0.0, None, ALU.max)
+            else:
+                nc.scalar.activation(z_bf16[:], diff[:].rearrange("p s v -> p v s"), ACT.Relu)
+            z_codes = keep.tile([P, n], U32, name=f"z_codes{c}", align_bytes=64)
+            z_plane = keep.tile([P, n], U8, name=f"z_plane{c}", align_bytes=64)
+            nc.vector.quantize_mx(out=z_codes[:].bitcast(FP8X4), scales=z_plane[:], in_=z_bf16[:].rearrange("p v s -> p (v s)"))
+            acc = psum.tile([P, n], F32, name=f"acc{c}", tag=f"bank{c // 2}{c % 2}")
+            nc.tensor.matmul_mx(
+                out=acc[:],
+                lhsT=w2_codes[:].bitcast(FP8X4),
+                lhsT_scale=w2_plane[:],
+                rhs=z_codes[:].bitcast(FP8X4),
+                rhs_scale=z_plane[:],
+                start=True,
+                stop=True,
+            )
+            result = keep.tile([P, n], F32, name=f"result{c}")
+            nc.scalar.copy(result[:], acc[:])
+            nc.sync.dma_start(out[:, v0:v1], result[:])
+
+        diff = keep.tile([P, PACK, PAIR_CHUNKS[0][1]], F32, name="diff0")
+        for s in range(PACK):
+            fetch_right(s)
+            subtract(diff, s, 0)
+        second_layer(diff, 0)
+        for c in range(1, len(PAIR_CHUNKS)):
+            v0, v1 = PAIR_CHUNKS[c]
+            diff = keep.tile([P, PACK, v1 - v0], F32, name=f"diff{c}", tag=f"handed_on{c - 1}")
+            for s in range(PACK):
+                subtract(diff, s, c)
+            second_layer(diff, c)

@@ -21,7 +21,8 @@ K_PASS = P * PACK
 PASSES = K // K_PASS
 BANK = 512
 PER_COLUMN = 16
-PAIR_CHUNKS = ((0, 256), (256, 384), (384, 512))
+EARLY = 256
+PAIR_CHUNKS = ((0, EARLY), (EARLY, 384), (384, V))
 
 
 def tile_picked_phpair_relu_p_kernel(tc, x_words, x_scales, w1, w2_words, w2_scales, offs, left, right, out):
@@ -36,54 +37,53 @@ def tile_picked_phpair_relu_p_kernel(tc, x_words, x_scales, w1, w2_words, w2_sca
         left_sb = lists.tile([P, V // PER_COLUMN], U16, name="left_sb")
         right_sb = lists.tile([P, V // PER_COLUMN], U16, name="right_sb")
         nc.sync.dma_start(offs_sb[:], offs)
+        nc.sync.dma_start(left_sb[:], left)
+        nc.sync.dma_start(right_sb[:], right)
 
-        scale_table = shared.tile([P, T], U8, name="scale_table", align_bytes=64, offset=4 * T - T // 2)
+        scale_table = keep.tile([P, T], U8, name="scale_table", align_bytes=64)
         nc.gpsimd.memset(scale_table[:].bitcast(I32), 0)
-        rows = x_scales.bitcast(I32).rearrange("z (r j) c -> j r z c", j=2)
-        for j in range(2):
-            nc.scalar.dma_start(scale_table[j:P:8, :].bitcast(I32), rows[j])
 
-        word_table = [
-            keep.tile([P, T], I32, name="word_table0", align_bytes=64),
-            shared.tile([P, T], I32, name="word_table1", align_bytes=64, offset=0),
-        ]
+        word_table = [keep.tile([P, T], I32, name=f"word_table{z}", align_bytes=64) for z in range(PASSES)]
         w_first = keep.tile([P, PACK, H], F32, name="w_first")
-        w_halves = shared.tile([P, 2, PACK, H // 2], F32, name="w_halves", align_bytes=64, offset=4 * T)
+        w_halves = shared.tile([P, 2, PACK, H // 2], F32, name="w_halves", align_bytes=64, offset=0)
         w_second = [w_halves[:, u, :, :] for u in range(2)]
         w1_rows = w1.rearrange("(z p t) c -> z p t c", z=PASSES, t=PACK)
 
-        def load_words(z):
-            nc.sync.dma_start(word_table[z][:], x_words[z].rearrange("p n t -> p (n t)").bitcast(I32))
+        def load_words(z, c0, c1):
+            nc.sync.dma_start(word_table[z][:, c0:c1], x_words[z].rearrange("p n t -> p (n t)").bitcast(I32)[:, c0:c1])
 
-        load_words(0)
-        nc.sync.dma_start(left_sb[:], left)
-        nc.sync.dma_start(right_sb[:], right)
+        load_words(0, 0, T // 4)
+        rows = x_scales.bitcast(I32).rearrange("z (r j) c -> j r z c", j=2)
+        for j in range(2):
+            nc.sync.dma_start(scale_table[j:P:8, :].bitcast(I32), rows[j])
+        load_words(0, T // 4, T)
         nc.sync.dma_start(w_first[:], w1_rows[0])
+        load_words(1, 0, T)
 
         w2_codes = keep.tile([P, N], I32, name="w2_codes", align_bytes=64)
         w2_plane = keep.tile([P, N], U8, name="w2_plane", align_bytes=64)
-        nc.gpsimd.memset(w2_plane[:], 0)
+        nc.vector.memset(w2_plane[:].bitcast(I32), 0)
         nc.gpsimd.dma_start(w2_codes[:], w2_words[0].rearrange("p n t -> p (n t)").bitcast(I32))
         for q in range(4):
             nc.gpsimd.dma_start(w2_plane[32 * q : 32 * q + 4, :].bitcast(I32), w2_scales[0].bitcast(I32)[4 * q : 4 * q + 4, :])
 
-        picked_scales = keep.tile([P, S], U8, name="picked_scales", align_bytes=64)
+        picked_scales = shared.tile([P, S], U8, name="picked_scales", align_bytes=64, offset=0)
         x_plane = keep.tile([P, S], U8, name="x_plane", align_bytes=64)
         nc.vector.tensor_copy(picked_scales[:], scale_table[:].indirect(offs_sb[:]))
-        load_words(1)
-        for u in range(2):
-            nc.sync.dma_start(w_second[u], w1_rows[1][:, :, u * (H // 2) : (u + 1) * (H // 2)])
         nc.vector.tensor_copy(x_plane[:].bitcast(I32), picked_scales[:].bitcast(I32))
         for z in range(PASSES):
             for j in range(2):
-                nc.scalar.dma_start(
+                nc.sync.dma_start(
                     x_plane[8 * z + 2 + j : P : 32, :].bitcast(I32),
-                    picked_scales[16 + 8 * z + j : P : 32, :].bitcast(I32),
+                    x_plane[16 + 8 * z + j : P : 32, :].bitcast(I32),
                 )
+        for u in range(2):
+            nc.sync.dma_start(w_second[u], w1_rows[1][:, :, u * (H // 2) : (u + 1) * (H // 2)])
 
-        x_codes = [keep.tile([P, S], U32, name=f"x_codes{z}", align_bytes=64) for z in range(PASSES)]
+        x_codes = [None] * PASSES
 
-        def pick_words(z):
+        def pick_words(z, tag):
+            x_codes[z] = keep.tile([P, S], U32, name=f"x_codes{z}", tag=tag, align_bytes=64)
             nc.vector.tensor_copy(x_codes[z][:], word_table[z][:].bitcast(U32).indirect(offs_sb[:]))
 
         w_bf16 = [[keep.tile([P, 2, P, PACK], BF16, name=f"w_bf16_{z}{d}", align_bytes=64) for d in range(2)] for z in range(PASSES)]
@@ -126,11 +126,11 @@ def tile_picked_phpair_relu_p_kernel(tc, x_words, x_scales, w1, w2_words, w2_sca
                     stop=(z == PASSES - 1),
                 )
 
-        pick_words(0)
+        pick_words(0, "x_codes0")
         for d in range(2):
             deal_on_scalar(0, d, w_first[:], 0, P)
         quantize_w(0, 0, 0, 2)
-        pick_words(1)
+        pick_words(1, "w_bf16_00")
         for d in range(2):
             deal_on_scalar(1, d, w_second[0], 0, P // 2)
         deal_on_vector(1, 0, w_second[1], P // 2, P)
@@ -139,11 +139,7 @@ def tile_picked_phpair_relu_p_kernel(tc, x_words, x_scales, w1, w2_words, w2_sca
         quantize_w(1, 0, 1, 2)
         quantize_w(0, 1, 0, 2)
         quantize_w(1, 1, 0, 2)
-        for s in range(2):
-            first_layer_pass(0, s)
-        for s in range(2):
-            first_layer_pass(1, s)
-        for s in range(2, PACK):
+        for s in range(PACK):
             for z in range(PASSES):
                 first_layer_pass(z, s)
 
@@ -154,26 +150,23 @@ def tile_picked_phpair_relu_p_kernel(tc, x_words, x_scales, w1, w2_words, w2_sca
             for u in range(2):
                 nc.scalar.copy(h[s][:, u * BANK : (u + 1) * BANK], banks[s][u][:])
 
-        def entries(index, c):
-            v0, v1 = PAIR_CHUNKS[c]
+        def entries(index, v0, v1):
             return index[:, v0 // PER_COLUMN : v1 // PER_COLUMN]
 
-        h_right = [[None] * len(PAIR_CHUNKS) for s in range(PACK)]
+        def fetch_right(s, v0, v1, tag):
+            fetched = keep.tile([P, v1 - v0], F32, name=f"h_right{s}_{v0}", tag=tag, align_bytes=64)
+            nc.vector.tensor_copy(fetched[:], h[s][:].indirect(entries(right_sb, v0, v1)))
+            return fetched
 
-        def fetch_right(s):
-            for c, (v0, v1) in enumerate(PAIR_CHUNKS):
-                tag = f"handed_on{c}" if s == PACK - 1 else f"h_right{s}{c}"
-                h_right[s][c] = keep.tile([P, v1 - v0], F32, name=f"h_right{s}{c}", tag=tag)
-                nc.vector.tensor_copy(h_right[s][c][:], h[s][:].indirect(entries(right_sb, c)))
-
-        def subtract(diff, s, c):
-            nc.vector.tensor_tensor(diff[:, s, :], h[s][:].indirect(entries(left_sb, c)), h_right[s][c][:], ALU.subtract)
+        def subtract(dst, s, v0, v1, fetched):
+            nc.vector.tensor_tensor(dst, h[s][:].indirect(entries(left_sb, v0, v1)), fetched, ALU.subtract)
 
         def second_layer(diff, c):
             v0, v1 = PAIR_CHUNKS[c]
             n = v1 - v0
+            last = c == len(PAIR_CHUNKS) - 1
             z_bf16 = keep.tile([P, n, PACK], BF16, name=f"z_bf16_{c}", align_bytes=64)
-            if c == len(PAIR_CHUNKS) - 1:
+            if last:
                 nc.vector.tensor_scalar(z_bf16[:], diff[:].rearrange("p s v -> p v s"), 0.0, None, ALU.max)
             else:
                 nc.scalar.activation(z_bf16[:], diff[:].rearrange("p s v -> p v s"), ACT.Relu)
@@ -191,17 +184,22 @@ def tile_picked_phpair_relu_p_kernel(tc, x_words, x_scales, w1, w2_words, w2_sca
                 stop=True,
             )
             result = keep.tile([P, n], F32, name=f"result{c}")
-            nc.scalar.copy(result[:], acc[:])
+            if last:
+                nc.vector.tensor_copy(result[:], acc[:])
+            else:
+                nc.scalar.copy(result[:], acc[:])
             nc.sync.dma_start(out[:, v0:v1], result[:])
 
-        diff = keep.tile([P, PACK, PAIR_CHUNKS[0][1]], F32, name="diff0")
+        diff = keep.tile([P, PACK, EARLY], F32, name="diff0")
+        late_right = []
         for s in range(PACK):
-            fetch_right(s)
-            subtract(diff, s, 0)
+            fetched = fetch_right(s, 0, EARLY, f"early_right{s}")
+            late_right.append(fetch_right(s, EARLY, V, f"late_right{s}"))
+            subtract(diff[:, s, :], s, 0, EARLY, fetched[:])
         second_layer(diff, 0)
-        for c in range(1, len(PAIR_CHUNKS)):
+        for c, tag in ((1, f"early_right{PACK - 1}"), (2, "z_bf16_0")):
             v0, v1 = PAIR_CHUNKS[c]
-            diff = keep.tile([P, PACK, v1 - v0], F32, name=f"diff{c}", tag=f"handed_on{c - 1}")
+            diff = keep.tile([P, PACK, v1 - v0], F32, name=f"diff{c}", tag=tag, align_bytes=64)
             for s in range(PACK):
-                subtract(diff, s, c)
+                subtract(diff[:, s, :], s, v0, v1, late_right[s][:, v0 - EARLY : v1 - EARLY])
             second_layer(diff, c)

@@ -21,8 +21,8 @@ K_PASS = P * PACK
 PASSES = K // K_PASS
 BANK = 512
 PER_COLUMN = 16
-EARLY = 256
-PAIR_CHUNKS = ((0, EARLY), (EARLY, 384), (384, V))
+EARLY = 320
+PAIR_CHUNKS = ((0, 256), (256, EARLY), (EARLY, 448), (448, V))
 
 
 def tile_picked_phpair_relu_p_kernel(tc, x_words, x_scales, w1, w2_words, w2_scales, offs, left, right, out):
@@ -60,14 +60,7 @@ def tile_picked_phpair_relu_p_kernel(tc, x_words, x_scales, w1, w2_words, w2_sca
         nc.sync.dma_start(w_first[:], w1_rows[0])
         load_words(1, 0, T)
 
-        w2_codes = keep.tile([P, N], I32, name="w2_codes", align_bytes=64)
-        w2_plane = keep.tile([P, N], U8, name="w2_plane", align_bytes=64)
-        nc.vector.memset(w2_plane[:].bitcast(I32), 0)
-        nc.gpsimd.dma_start(w2_codes[:], w2_words[0].rearrange("p n t -> p (n t)").bitcast(I32))
-        for q in range(4):
-            nc.gpsimd.dma_start(w2_plane[32 * q : 32 * q + 4, :].bitcast(I32), w2_scales[0].bitcast(I32)[4 * q : 4 * q + 4, :])
-
-        picked_scales = shared.tile([P, S], U8, name="picked_scales", align_bytes=64, offset=0)
+        picked_scales = shared.tile([P, S], U8, name="picked_scales", align_bytes=64, offset=8192 - 256)
         x_plane = keep.tile([P, S], U8, name="x_plane", align_bytes=64)
         nc.vector.tensor_copy(picked_scales[:], scale_table[:].indirect(offs_sb[:]))
         nc.vector.tensor_copy(x_plane[:].bitcast(I32), picked_scales[:].bitcast(I32))
@@ -80,6 +73,13 @@ def tile_picked_phpair_relu_p_kernel(tc, x_words, x_scales, w1, w2_words, w2_sca
         for u in range(2):
             nc.sync.dma_start(w_second[u], w1_rows[1][:, :, u * (H // 2) : (u + 1) * (H // 2)])
 
+        w2_plane = shared.tile([P, N], U8, name="w2_plane", align_bytes=64, offset=8192)
+        w2_codes = shared.tile([P, N], I32, name="w2_codes", align_bytes=64, offset=8192 + N)
+        nc.gpsimd.memset(w2_plane[:].bitcast(I32), 0)
+        nc.sync.dma_start(w2_codes[:], w2_words[0].rearrange("p n t -> p (n t)").bitcast(I32))
+        for q in range(4):
+            nc.sync.dma_start(w2_plane[32 * q : 32 * q + 4, :].bitcast(I32), w2_scales[0].bitcast(I32)[4 * q : 4 * q + 4, :])
+
         x_codes = [None] * PASSES
 
         def pick_words(z, tag):
@@ -91,8 +91,8 @@ def tile_picked_phpair_relu_p_kernel(tc, x_words, x_scales, w1, w2_words, w2_sca
         w_plane = [[keep.tile([P, 2 * P], U8, name=f"w_plane{z}{d}", align_bytes=64) for d in range(2)] for z in range(PASSES)]
 
         def deal_views(z, d, raw, m0, m1):
-            dst = w_bf16[z][d][:, :, m0:m1, :].rearrange("p s m t -> p m s t")
-            src = raw.rearrange("p t (m s) -> p m s t", s=PACK)[:, :, 2 * d : 2 * d + 2, :]
+            dst = w_bf16[z][d][:, :, m0:m1, :].rearrange("p s m t -> p m t s")
+            src = raw.rearrange("p t (m s) -> p m t s", s=PACK)[:, :, :, 2 * d : 2 * d + 2]
             return dst, src
 
         def deal_on_scalar(z, d, raw, m0, m1):
@@ -110,14 +110,18 @@ def tile_picked_phpair_relu_p_kernel(tc, x_words, x_scales, w1, w2_words, w2_sca
                 in_=w_bf16[z][d][:, s0:s1, :, :].rearrange("p s m t -> p (s m t)"),
             )
 
-        banks = [[psum.tile([P, BANK], F32, name=f"bank{s}{u}") for u in range(2)] for s in range(PACK)]
+        widths = [BANK // 2] + [BANK] * (PACK - 1)
+        sums = [None] * PACK
+
+        def open_sums(s, first_bank):
+            sums[s] = [psum.tile([P, widths[s]], F32, name=f"sums{s}{u}", tag=f"bank{first_bank + u}") for u in range(S // widths[s])]
 
         def first_layer_pass(z, s):
             d, cols = s // 2, slice((s % 2) * P, (s % 2 + 1) * P)
-            for u in range(2):
-                places = slice(u * BANK, (u + 1) * BANK)
+            for u, acc in enumerate(sums[s]):
+                places = slice(u * widths[s], (u + 1) * widths[s])
                 nc.tensor.matmul_mx(
-                    out=banks[s][u][:],
+                    out=acc[:],
                     lhsT=w_codes[z][d][:, cols].bitcast(FP8X4),
                     lhsT_scale=w_plane[z][d][:, cols],
                     rhs=x_codes[z][:, places].bitcast(FP8X4),
@@ -131,24 +135,25 @@ def tile_picked_phpair_relu_p_kernel(tc, x_words, x_scales, w1, w2_words, w2_sca
             deal_on_scalar(0, d, w_first[:], 0, P)
         quantize_w(0, 0, 0, 2)
         pick_words(1, "w_bf16_00")
+        quantize_w(0, 1, 0, 2)
         for d in range(2):
             deal_on_scalar(1, d, w_second[0], 0, P // 2)
         deal_on_vector(1, 0, w_second[1], P // 2, P)
         deal_on_scalar(1, 1, w_second[1], P // 2, P)
         quantize_w(1, 0, 0, 1)
         quantize_w(1, 0, 1, 2)
-        quantize_w(0, 1, 0, 2)
         quantize_w(1, 1, 0, 2)
-        for s in range(PACK):
+        h = [keep.tile([P, S], F32, name=f"h{s}") for s in range(PACK)]
+        for s, first_bank in enumerate((0, 4, 6, 0)):
+            open_sums(s, first_bank)
             for z in range(PASSES):
                 first_layer_pass(z, s)
-
-        h = [keep.tile([P, S], F32, name=f"h{s}") for s in range(PACK)]
-        nc.scalar.copy(h[0][:, :BANK], banks[0][0][:])
-        nc.vector.tensor_copy(h[0][:, BANK:], banks[0][1][:])
-        for s in range(1, PACK):
-            for u in range(2):
-                nc.scalar.copy(h[s][:, u * BANK : (u + 1) * BANK], banks[s][u][:])
+            for u, acc in enumerate(sums[s]):
+                places = h[s][:, u * widths[s] : (u + 1) * widths[s]]
+                if s == 0 and u % 2 == 1:
+                    nc.vector.tensor_copy(places, acc[:])
+                else:
+                    nc.scalar.copy(places, acc[:])
 
         def entries(index, v0, v1):
             return index[:, v0 // PER_COLUMN : v1 // PER_COLUMN]
@@ -166,14 +171,16 @@ def tile_picked_phpair_relu_p_kernel(tc, x_words, x_scales, w1, w2_words, w2_sca
             n = v1 - v0
             last = c == len(PAIR_CHUNKS) - 1
             z_bf16 = keep.tile([P, n, PACK], BF16, name=f"z_bf16_{c}", align_bytes=64)
+            dst = z_bf16[:].rearrange("p (c i) s -> p c s i", i=4)
+            src = diff.rearrange("p s (c i) -> p c s i", i=4)
             if last:
-                nc.vector.tensor_scalar(z_bf16[:], diff[:].rearrange("p s v -> p v s"), 0.0, None, ALU.max)
+                nc.vector.tensor_scalar(dst, src, 0.0, None, ALU.max)
             else:
-                nc.scalar.activation(z_bf16[:], diff[:].rearrange("p s v -> p v s"), ACT.Relu)
+                nc.scalar.activation(dst, src, ACT.Relu)
             z_codes = keep.tile([P, n], U32, name=f"z_codes{c}", align_bytes=64)
             z_plane = keep.tile([P, n], U8, name=f"z_plane{c}", align_bytes=64)
             nc.vector.quantize_mx(out=z_codes[:].bitcast(FP8X4), scales=z_plane[:], in_=z_bf16[:].rearrange("p v s -> p (v s)"))
-            acc = psum.tile([P, n], F32, name=f"acc{c}", tag=f"bank{c // 2}{c % 2}")
+            acc = psum.tile([P, n], F32, name=f"acc{c}", tag=f"bank{2 + c}")
             nc.tensor.matmul_mx(
                 out=acc[:],
                 lhsT=w2_codes[:].bitcast(FP8X4),
@@ -196,10 +203,12 @@ def tile_picked_phpair_relu_p_kernel(tc, x_words, x_scales, w1, w2_words, w2_sca
             fetched = fetch_right(s, 0, EARLY, f"early_right{s}")
             late_right.append(fetch_right(s, EARLY, V, f"late_right{s}"))
             subtract(diff[:, s, :], s, 0, EARLY, fetched[:])
-        second_layer(diff, 0)
-        for c, tag in ((1, f"early_right{PACK - 1}"), (2, "z_bf16_0")):
+        for c in range(2):
+            v0, v1 = PAIR_CHUNKS[c]
+            second_layer(diff[:, :, v0:v1], c)
+        for c, tag in ((2, f"early_right{PACK - 1}"), (3, "z_bf16_0")):
             v0, v1 = PAIR_CHUNKS[c]
             diff = keep.tile([P, PACK, v1 - v0], F32, name=f"diff{c}", tag=tag, align_bytes=64)
             for s in range(PACK):
                 subtract(diff[:, s, :], s, v0, v1, late_right[s][:, v0 - EARLY : v1 - EARLY])
-            second_layer(diff, c)
+            second_layer(diff[:], c)

@@ -17,12 +17,21 @@ ACT = mybir.ActivationFunctionType
 
 P = 128
 PACK = 4
-K_PASS = P * PACK
-PASSES = K // K_PASS
+PASSES = K // (P * PACK)
 BANK = 512
-PER_COLUMN = 16
+GROUP = 16
+QUADRANT = 32
+LINE = 4
+PASS_ROW = 8
+
+FIRST_TOKENS = 3 * T // 8
+
 EARLY = 320
 PAIR_CHUNKS = ((0, 256), (256, EARLY), (EARLY, 448), (448, V))
+
+PLACES_PER_BANK = (BANK // 2, BANK, BANK, BANK)
+FIRST_BANK = (0, 4, 6, 0)
+FIRST_OUT_BANK = 2
 
 
 def tile_picked_phpair_relu_p_kernel(tc, x_words, x_scales, w1, w2_words, w2_scales, offs, left, right, out):
@@ -30,159 +39,163 @@ def tile_picked_phpair_relu_p_kernel(tc, x_words, x_scales, w1, w2_words, w2_sca
     with ExitStack() as ctx:
         lists = ctx.enter_context(tc.tile_pool(name="lists", bufs=1))
         keep = ctx.enter_context(tc.tile_pool(name="keep", bufs=1))
-        shared = ctx.enter_context(tc.tile_pool(name="shared", bufs=1))
+        placed = ctx.enter_context(tc.tile_pool(name="placed", bufs=1))
         psum = ctx.enter_context(tc.psum_pool(name="psum", bufs=1))
 
-        offs_sb = lists.tile([P, S // PER_COLUMN], U16, name="offs_sb")
-        left_sb = lists.tile([P, V // PER_COLUMN], U16, name="left_sb")
-        right_sb = lists.tile([P, V // PER_COLUMN], U16, name="right_sb")
-        nc.sync.dma_start(offs_sb[:], offs)
-        nc.sync.dma_start(left_sb[:], left)
-        nc.sync.dma_start(right_sb[:], right)
+        offs_sb = lists.tile([P, S // GROUP], U16, name="offs_sb")
+        left_sb = lists.tile([P, V // GROUP], U16, name="left_sb")
+        right_sb = lists.tile([P, V // GROUP], U16, name="right_sb")
 
         scale_table = keep.tile([P, T], U8, name="scale_table", align_bytes=64)
         nc.gpsimd.memset(scale_table[:].bitcast(I32), 0)
 
-        word_table = [keep.tile([P, T], I32, name=f"word_table{z}", align_bytes=64) for z in range(PASSES)]
-        w_first = keep.tile([P, PACK, H], F32, name="w_first")
-        w_halves = shared.tile([P, 2, PACK, H // 2], F32, name="w_halves", align_bytes=64, offset=0)
-        w_second = [w_halves[:, u, :, :] for u in range(2)]
-        w1_rows = w1.rearrange("(z p t) c -> z p t c", z=PASSES, t=PACK)
+        word_table = [keep.tile([P, T], I32, name=f"word_table{g}", align_bytes=64) for g in range(PASSES)]
+        w1_rows = w1.rearrange("(g p t) c -> g p t c", g=PASSES, t=PACK)
+        w1_first = keep.tile([P, PACK, H], F32, name="w1_first")
 
-        def load_words(z, c0, c1):
-            nc.sync.dma_start(word_table[z][:, c0:c1], x_words[z].rearrange("p n t -> p (n t)").bitcast(I32)[:, c0:c1])
+        def load_words(g, c0, c1):
+            nc.sync.dma_start(word_table[g][:, c0:c1], x_words[g].rearrange("p n t -> p (n t)").bitcast(I32)[:, c0:c1])
 
-        load_words(0, 0, T // 4)
-        rows = x_scales.bitcast(I32).rearrange("z (r j) c -> j r z c", j=2)
+        load_words(0, 0, FIRST_TOKENS)
+        nc.sync.dma_start(offs_sb[:], offs)
+        nc.sync.dma_start(left_sb[:], left)
+        nc.sync.dma_start(right_sb[:], right)
+        scale_rows = x_scales.bitcast(I32).rearrange("g (r j) c -> j r g c", j=2)
         for j in range(2):
-            nc.sync.dma_start(scale_table[j:P:8, :].bitcast(I32), rows[j])
-        load_words(0, T // 4, T)
-        nc.sync.dma_start(w_first[:], w1_rows[0])
+            nc.sync.dma_start(scale_table[j:P:PASS_ROW, :].bitcast(I32), scale_rows[j])
+        load_words(0, FIRST_TOKENS, T)
+        nc.sync.dma_start(w1_first[:], w1_rows[0])
         load_words(1, 0, T)
 
-        picked_scales = shared.tile([P, S], U8, name="picked_scales", align_bytes=64, offset=8192 - 256)
+        w1_second_bytes = 4 * PACK * H
+        w1_second = placed.tile([P, 2, PACK, H // 2], F32, name="w1_second", align_bytes=64, offset=0)
+        picked_scales = placed.tile([P, S], U8, name="picked_scales", align_bytes=64, offset=w1_second_bytes - S // 4)
         x_plane = keep.tile([P, S], U8, name="x_plane", align_bytes=64)
         nc.vector.tensor_copy(picked_scales[:], scale_table[:].indirect(offs_sb[:]))
         nc.vector.tensor_copy(x_plane[:].bitcast(I32), picked_scales[:].bitcast(I32))
-        for z in range(PASSES):
+        for g in range(PASSES):
             for j in range(2):
                 nc.sync.dma_start(
-                    x_plane[8 * z + 2 + j : P : 32, :].bitcast(I32),
-                    x_plane[16 + 8 * z + j : P : 32, :].bitcast(I32),
+                    x_plane[PASS_ROW * g + 2 + j : P : QUADRANT, :].bitcast(I32),
+                    x_plane[GROUP + PASS_ROW * g + j : P : QUADRANT, :].bitcast(I32),
                 )
         for u in range(2):
-            nc.sync.dma_start(w_second[u], w1_rows[1][:, :, u * (H // 2) : (u + 1) * (H // 2)])
+            nc.sync.dma_start(w1_second[:, u, :, :], w1_rows[1][:, :, u * (H // 2) : (u + 1) * (H // 2)])
 
-        w2_plane = shared.tile([P, N], U8, name="w2_plane", align_bytes=64, offset=8192)
-        w2_codes = shared.tile([P, N], I32, name="w2_codes", align_bytes=64, offset=8192 + N)
+        w2_plane = placed.tile([P, N], U8, name="w2_plane", align_bytes=64, offset=w1_second_bytes)
+        w2_codes = placed.tile([P, N], I32, name="w2_codes", align_bytes=64, offset=w1_second_bytes + N)
         nc.gpsimd.memset(w2_plane[:].bitcast(I32), 0)
         nc.sync.dma_start(w2_codes[:], w2_words[0].rearrange("p n t -> p (n t)").bitcast(I32))
-        for q in range(4):
-            nc.sync.dma_start(w2_plane[32 * q : 32 * q + 4, :].bitcast(I32), w2_scales[0].bitcast(I32)[4 * q : 4 * q + 4, :])
+        for q in range(P // QUADRANT):
+            nc.sync.dma_start(
+                w2_plane[QUADRANT * q : QUADRANT * q + 4, :].bitcast(I32),
+                w2_scales[0].bitcast(I32)[4 * q : 4 * q + 4, :],
+            )
 
         x_codes = [None] * PASSES
 
-        def pick_words(z, tag):
-            x_codes[z] = keep.tile([P, S], U32, name=f"x_codes{z}", tag=tag, align_bytes=64)
-            nc.vector.tensor_copy(x_codes[z][:], word_table[z][:].bitcast(U32).indirect(offs_sb[:]))
+        def pick_words(g, tag):
+            x_codes[g] = keep.tile([P, S], U32, name=f"x_codes{g}", tag=tag, align_bytes=64)
+            nc.vector.tensor_copy(x_codes[g][:], word_table[g][:].bitcast(U32).indirect(offs_sb[:]))
 
-        w_bf16 = [[keep.tile([P, 2, P, PACK], BF16, name=f"w_bf16_{z}{d}", align_bytes=64) for d in range(2)] for z in range(PASSES)]
-        w_codes = [[keep.tile([P, 2 * P], U32, name=f"w_codes{z}{d}", align_bytes=64) for d in range(2)] for z in range(PASSES)]
-        w_plane = [[keep.tile([P, 2 * P], U8, name=f"w_plane{z}{d}", align_bytes=64) for d in range(2)] for z in range(PASSES)]
+        w1_bf16 = [[keep.tile([P, 2, P, PACK], BF16, name=f"w1_bf16_{g}{d}", align_bytes=64) for d in range(2)] for g in range(PASSES)]
+        w1_codes = [[None] * 2 for g in range(PASSES)]
+        w1_plane = [[keep.tile([P, 2 * P], U8, name=f"w1_plane{g}{d}", align_bytes=64) for d in range(2)] for g in range(PASSES)]
 
-        def deal_views(z, d, raw, m0, m1):
-            dst = w_bf16[z][d][:, :, m0:m1, :].rearrange("p s m t -> p m t s")
+        def deal_views(g, d, raw, m0, m1):
+            dst = w1_bf16[g][d][:, :, m0:m1, :].rearrange("p e m t -> p m t e")
             src = raw.rearrange("p t (m s) -> p m t s", s=PACK)[:, :, :, 2 * d : 2 * d + 2]
             return dst, src
 
-        def deal_on_scalar(z, d, raw, m0, m1):
-            dst, src = deal_views(z, d, raw, m0, m1)
+        def deal_on_scalar(g, d, raw, m0, m1):
+            dst, src = deal_views(g, d, raw, m0, m1)
             nc.scalar.copy(dst, src)
 
-        def deal_on_vector(z, d, raw, m0, m1):
-            dst, src = deal_views(z, d, raw, m0, m1)
+        def deal_on_vector(g, d, raw, m0, m1):
+            dst, src = deal_views(g, d, raw, m0, m1)
             nc.vector.tensor_copy(dst, src)
 
-        def quantize_w(z, d, s0, s1):
+        def open_w1_codes(g, d, tag):
+            w1_codes[g][d] = keep.tile([P, 2 * P], U32, name=f"w1_codes{g}{d}", tag=tag, align_bytes=64)
+
+        def quantize_w1(g, d, e0, e1):
             nc.vector.quantize_mx(
-                out=w_codes[z][d][:, s0 * P : s1 * P].bitcast(FP8X4),
-                scales=w_plane[z][d][:, s0 * P : s1 * P],
-                in_=w_bf16[z][d][:, s0:s1, :, :].rearrange("p s m t -> p (s m t)"),
+                out=w1_codes[g][d][:, e0 * P : e1 * P].bitcast(FP8X4),
+                scales=w1_plane[g][d][:, e0 * P : e1 * P],
+                in_=w1_bf16[g][d][:, e0:e1, :, :].rearrange("p e m t -> p (e m t)"),
             )
-
-        widths = [BANK // 2] + [BANK] * (PACK - 1)
-        sums = [None] * PACK
-
-        def open_sums(s, first_bank):
-            sums[s] = [psum.tile([P, widths[s]], F32, name=f"sums{s}{u}", tag=f"bank{first_bank + u}") for u in range(S // widths[s])]
-
-        def first_layer_pass(z, s):
-            d, cols = s // 2, slice((s % 2) * P, (s % 2 + 1) * P)
-            for u, acc in enumerate(sums[s]):
-                places = slice(u * widths[s], (u + 1) * widths[s])
-                nc.tensor.matmul_mx(
-                    out=acc[:],
-                    lhsT=w_codes[z][d][:, cols].bitcast(FP8X4),
-                    lhsT_scale=w_plane[z][d][:, cols],
-                    rhs=x_codes[z][:, places].bitcast(FP8X4),
-                    rhs_scale=x_plane[8 * z : P, places],
-                    start=(z == 0),
-                    stop=(z == PASSES - 1),
-                )
 
         pick_words(0, "x_codes0")
         for d in range(2):
-            deal_on_scalar(0, d, w_first[:], 0, P)
-        quantize_w(0, 0, 0, 2)
-        pick_words(1, "w_bf16_00")
-        quantize_w(0, 1, 0, 2)
+            deal_on_scalar(0, d, w1_first[:], 0, P)
+        open_w1_codes(0, 0, "w1_codes00")
+        quantize_w1(0, 0, 0, 2)
+        pick_words(1, "w1_bf16_00")
         for d in range(2):
-            deal_on_scalar(1, d, w_second[0], 0, P // 2)
-        deal_on_vector(1, 0, w_second[1], P // 2, P)
-        deal_on_scalar(1, 1, w_second[1], P // 2, P)
-        quantize_w(1, 0, 0, 1)
-        quantize_w(1, 0, 1, 2)
-        quantize_w(1, 1, 0, 2)
+            deal_on_scalar(1, d, w1_second[:, 0, :, :], 0, P // 2)
+        last_quarters = w1_second[:, 1, :, :].rearrange("p t (u c) -> p t u c", u=2)
+        deal_on_vector(1, 0, last_quarters[:, :, 0, :], P // 2, 3 * P // 4)
+        deal_on_scalar(1, 0, last_quarters[:, :, 1, :], 3 * P // 4, P)
+        deal_on_scalar(1, 1, w1_second[:, 1, :, :], P // 2, P)
+        open_w1_codes(1, 0, "w1_codes10")
+        quantize_w1(1, 0, 0, 1)
+        quantize_w1(1, 0, 1, 2)
+        open_w1_codes(0, 1, "w1_bf16_10")
+        quantize_w1(0, 1, 0, 2)
+        open_w1_codes(1, 1, "w1_codes11")
+        quantize_w1(1, 1, 0, 2)
+
         h = [keep.tile([P, S], F32, name=f"h{s}") for s in range(PACK)]
-        for s, first_bank in enumerate((0, 4, 6, 0)):
-            open_sums(s, first_bank)
-            for z in range(PASSES):
-                first_layer_pass(z, s)
-            for u, acc in enumerate(sums[s]):
-                places = h[s][:, u * widths[s] : (u + 1) * widths[s]]
+        for s in range(PACK):
+            width = PLACES_PER_BANK[s]
+            sums = [psum.tile([P, width], F32, name=f"sums{s}{u}", tag=f"bank{FIRST_BANK[s] + u}") for u in range(S // width)]
+            d, columns = s // 2, slice((s % 2) * P, (s % 2 + 1) * P)
+            for g in range(PASSES):
+                for u, bank in enumerate(sums):
+                    places = slice(u * width, (u + 1) * width)
+                    nc.tensor.matmul_mx(
+                        out=bank[:],
+                        lhsT=w1_codes[g][d][:, columns].bitcast(FP8X4),
+                        lhsT_scale=w1_plane[g][d][:, columns],
+                        rhs=x_codes[g][:, places].bitcast(FP8X4),
+                        rhs_scale=x_plane[PASS_ROW * g : P, places],
+                        start=(g == 0),
+                        stop=(g == PASSES - 1),
+                    )
+            for u, bank in enumerate(sums):
                 if s == 0 and u % 2 == 1:
-                    nc.vector.tensor_copy(places, acc[:])
+                    nc.vector.tensor_copy(h[s][:, u * width : (u + 1) * width], bank[:])
                 else:
-                    nc.scalar.copy(places, acc[:])
+                    nc.scalar.copy(h[s][:, u * width : (u + 1) * width], bank[:])
 
-        def entries(index, v0, v1):
-            return index[:, v0 // PER_COLUMN : v1 // PER_COLUMN]
+        def entries(list_sb, v0, v1):
+            return list_sb[:, v0 // GROUP : v1 // GROUP]
 
-        def fetch_right(s, v0, v1, tag):
-            fetched = keep.tile([P, v1 - v0], F32, name=f"h_right{s}_{v0}", tag=tag, align_bytes=64)
-            nc.vector.tensor_copy(fetched[:], h[s][:].indirect(entries(right_sb, v0, v1)))
-            return fetched
+        def fetch_right(s, v0, v1, name):
+            h_right = keep.tile([P, v1 - v0], F32, name=name, align_bytes=64)
+            nc.vector.tensor_copy(h_right[:], h[s][:].indirect(entries(right_sb, v0, v1)))
+            return h_right
 
-        def subtract(dst, s, v0, v1, fetched):
-            nc.vector.tensor_tensor(dst, h[s][:].indirect(entries(left_sb, v0, v1)), fetched, ALU.subtract)
+        def subtract(dst, s, v0, v1, h_right):
+            nc.vector.tensor_tensor(dst, h[s][:].indirect(entries(left_sb, v0, v1)), h_right, ALU.subtract)
 
         def second_layer(diff, c):
             v0, v1 = PAIR_CHUNKS[c]
-            n = v1 - v0
+            pairs = v1 - v0
             last = c == len(PAIR_CHUNKS) - 1
-            z_bf16 = keep.tile([P, n, PACK], BF16, name=f"z_bf16_{c}", align_bytes=64)
-            dst = z_bf16[:].rearrange("p (c i) s -> p c s i", i=4)
-            src = diff.rearrange("p s (c i) -> p c s i", i=4)
+            z_bf16 = keep.tile([P, pairs, PACK], BF16, name=f"z_bf16_{c}", align_bytes=64)
+            dst = z_bf16[:].rearrange("p (a b) s -> p a s b", b=LINE)
+            src = diff.rearrange("p s (a b) -> p a s b", b=LINE)
             if last:
                 nc.vector.tensor_scalar(dst, src, 0.0, None, ALU.max)
             else:
                 nc.scalar.activation(dst, src, ACT.Relu)
-            z_codes = keep.tile([P, n], U32, name=f"z_codes{c}", align_bytes=64)
-            z_plane = keep.tile([P, n], U8, name=f"z_plane{c}", align_bytes=64)
+            z_codes = keep.tile([P, pairs], U32, name=f"z_codes{c}", align_bytes=64)
+            z_plane = keep.tile([P, pairs], U8, name=f"z_plane{c}", align_bytes=64)
             nc.vector.quantize_mx(out=z_codes[:].bitcast(FP8X4), scales=z_plane[:], in_=z_bf16[:].rearrange("p v s -> p (v s)"))
-            acc = psum.tile([P, n], F32, name=f"acc{c}", tag=f"bank{2 + c}")
+            out_sums = psum.tile([P, pairs], F32, name=f"out_sums{c}", tag=f"bank{FIRST_OUT_BANK + c}")
             nc.tensor.matmul_mx(
-                out=acc[:],
+                out=out_sums[:],
                 lhsT=w2_codes[:].bitcast(FP8X4),
                 lhsT_scale=w2_plane[:],
                 rhs=z_codes[:].bitcast(FP8X4),
@@ -190,25 +203,25 @@ def tile_picked_phpair_relu_p_kernel(tc, x_words, x_scales, w1, w2_words, w2_sca
                 start=True,
                 stop=True,
             )
-            result = keep.tile([P, n], F32, name=f"result{c}")
+            result = keep.tile([P, pairs], F32, name=f"result{c}")
             if last:
-                nc.vector.tensor_copy(result[:], acc[:])
+                nc.vector.tensor_copy(result[:], out_sums[:])
             else:
-                nc.scalar.copy(result[:], acc[:])
+                nc.scalar.copy(result[:], out_sums[:])
             nc.sync.dma_start(out[:, v0:v1], result[:])
 
-        diff = keep.tile([P, PACK, EARLY], F32, name="diff0")
+        early_diff = keep.tile([P, PACK, EARLY], F32, name="early_diff")
         late_right = []
         for s in range(PACK):
-            fetched = fetch_right(s, 0, EARLY, f"early_right{s}")
+            early_right = fetch_right(s, 0, EARLY, f"early_right{s}")
             late_right.append(fetch_right(s, EARLY, V, f"late_right{s}"))
-            subtract(diff[:, s, :], s, 0, EARLY, fetched[:])
+            subtract(early_diff[:, s, :], s, 0, EARLY, early_right[:])
         for c in range(2):
             v0, v1 = PAIR_CHUNKS[c]
-            second_layer(diff[:, :, v0:v1], c)
+            second_layer(early_diff[:, :, v0:v1], c)
         for c, tag in ((2, f"early_right{PACK - 1}"), (3, "z_bf16_0")):
             v0, v1 = PAIR_CHUNKS[c]
-            diff = keep.tile([P, PACK, v1 - v0], F32, name=f"diff{c}", tag=tag, align_bytes=64)
+            late_diff = keep.tile([P, PACK, v1 - v0], F32, name=f"late_diff{c}", tag=tag, align_bytes=64)
             for s in range(PACK):
-                subtract(diff[:, s, :], s, v0, v1, late_right[s][:, v0 - EARLY : v1 - EARLY])
-            second_layer(diff[:], c)
+                subtract(late_diff[:, s, :], s, v0, v1, late_right[s][:, v0 - EARLY : v1 - EARLY])
+            second_layer(late_diff[:], c)

@@ -21,7 +21,7 @@ PASSES = K // (P * PACK)
 BANK = 512
 GROUP = 16
 QUADRANT = 32
-LINE = 4
+LINE = 2
 PASS_ROW = 8
 
 FIRST_TOKENS = 3 * T // 8

@@ -133,9 +133,7 @@ def tile_picked_phpair_relu_p_kernel(tc, x_words, x_scales, w1, w2_words, w2_sca
         pick_words(1, "w1_bf16_00")
         for d in range(2):
             deal_on_scalar(1, d, w1_second[:, 0, :, :], 0, P // 2)
-        last_quarters = w1_second[:, 1, :, :].rearrange("p t (u c) -> p t u c", u=2)
-        deal_on_vector(1, 0, last_quarters[:, :, 0, :], P // 2, 3 * P // 4)
-        deal_on_scalar(1, 0, last_quarters[:, :, 1, :], 3 * P // 4, P)
+        deal_on_vector(1, 0, w1_second[:, 1, :, :], P // 2, P)
         deal_on_scalar(1, 1, w1_second[:, 1, :, :], P // 2, P)
         open_w1_codes(1, 0, "w1_codes10")
         quantize_w1(1, 0, 0, 1)

@@ -26,8 +26,8 @@ PASS_ROW = 8
 
 FIRST_TOKENS = 3 * T // 8
 
-EARLY = 320
-PAIR_CHUNKS = ((0, 256), (256, EARLY), (EARLY, 448), (448, V))
+HALF = V // 2
+PAIR_CHUNKS = ((0, 128), (128, 256), (256, 384), (384, V))
 
 PLACES_PER_BANK = (BANK // 2, BANK, BANK, BANK)
 FIRST_BANK = (0, 4, 6, 0)
@@ -144,12 +144,14 @@ def tile_picked_phpair_relu_p_kernel(tc, x_words, x_scales, w1, w2_words, w2_sca
         quantize_w1(1, 1, 0, 2)
 
         h = [keep.tile([P, S], F32, name=f"h{s}") for s in range(PACK)]
-        for s in range(PACK):
+        sums = [None] * PACK
+
+        def multiply(s):
             width = PLACES_PER_BANK[s]
-            sums = [psum.tile([P, width], F32, name=f"sums{s}{u}", tag=f"bank{FIRST_BANK[s] + u}") for u in range(S // width)]
+            sums[s] = [psum.tile([P, width], F32, name=f"sums{s}{u}", tag=f"bank{FIRST_BANK[s] + u}") for u in range(S // width)]
             d, columns = s // 2, slice((s % 2) * P, (s % 2 + 1) * P)
             for g in range(PASSES):
-                for u, bank in enumerate(sums):
+                for u, bank in enumerate(sums[s]):
                     places = slice(u * width, (u + 1) * width)
                     nc.tensor.matmul_mx(
                         out=bank[:],
@@ -160,37 +162,43 @@ def tile_picked_phpair_relu_p_kernel(tc, x_words, x_scales, w1, w2_words, w2_sca
                         start=(g == 0),
                         stop=(g == PASSES - 1),
                     )
-            for u, bank in enumerate(sums):
-                if s == 0 and u % 2 == 1:
-                    nc.vector.tensor_copy(h[s][:, u * width : (u + 1) * width], bank[:])
-                else:
-                    nc.scalar.copy(h[s][:, u * width : (u + 1) * width], bank[:])
+
+        def empty(s, u, on_vector):
+            width = PLACES_PER_BANK[s]
+            if on_vector:
+                nc.vector.tensor_copy(h[s][:, u * width : (u + 1) * width], sums[s][u][:])
+            else:
+                nc.scalar.copy(h[s][:, u * width : (u + 1) * width], sums[s][u][:])
 
         def entries(list_sb, v0, v1):
             return list_sb[:, v0 // GROUP : v1 // GROUP]
 
-        def fetch_right(s, v0, v1, name):
-            h_right = keep.tile([P, v1 - v0], F32, name=name, align_bytes=64)
-            nc.vector.tensor_copy(h_right[:], h[s][:].indirect(entries(right_sb, v0, v1)))
-            return h_right
+        def fetch_right(dst, s, v0, v1):
+            nc.scalar.activation(dst, h[s][:].indirect(entries(right_sb, v0, v1)), ACT.Copy)
 
-        def subtract(dst, s, v0, v1, h_right):
-            nc.vector.tensor_tensor(dst, h[s][:].indirect(entries(left_sb, v0, v1)), h_right, ALU.subtract)
+        diff = [keep.tile([P, PACK, HALF], F32, name=f"diff{a}", align_bytes=64) for a in range(2)]
 
-        def second_layer(diff, c):
-            v0, v1 = PAIR_CHUNKS[c]
-            pairs = v1 - v0
-            last = c == len(PAIR_CHUNKS) - 1
-            z_bf16 = keep.tile([P, pairs, PACK], BF16, name=f"z_bf16_{c}", align_bytes=64)
-            dst = z_bf16[:].rearrange("p (a b) s -> p a s b", b=LINE)
-            src = diff.rearrange("p s (a b) -> p a s b", b=LINE)
-            if last:
+        def subtract(s, v0, v1, h_right):
+            a = v0 // HALF
+            nc.vector.tensor_tensor(diff[a][:, s, v0 - a * HALF : v1 - a * HALF], h[s][:].indirect(entries(left_sb, v0, v1)), h_right, ALU.subtract)
+
+        z_bf16 = [keep.tile([P, v1 - v0, PACK], BF16, name=f"z_bf16_{c}", align_bytes=64) for c, (v0, v1) in enumerate(PAIR_CHUNKS)]
+
+        def rectify(c, v0, v1, on_vector):
+            a, first = v0 // HALF, PAIR_CHUNKS[c][0]
+            dst = z_bf16[c][:, v0 - first : v1 - first, :].rearrange("p (a b) s -> p a s b", b=LINE)
+            src = diff[a][:, :, v0 - a * HALF : v1 - a * HALF].rearrange("p s (a b) -> p a s b", b=LINE)
+            if on_vector:
                 nc.vector.tensor_scalar(dst, src, 0.0, None, ALU.max)
             else:
                 nc.scalar.activation(dst, src, ACT.Relu)
+
+        def second_product(c, on_vector):
+            v0, v1 = PAIR_CHUNKS[c]
+            pairs = v1 - v0
             z_codes = keep.tile([P, pairs], U32, name=f"z_codes{c}", align_bytes=64)
             z_plane = keep.tile([P, pairs], U8, name=f"z_plane{c}", align_bytes=64)
-            nc.vector.quantize_mx(out=z_codes[:].bitcast(FP8X4), scales=z_plane[:], in_=z_bf16[:].rearrange("p v s -> p (v s)"))
+            nc.vector.quantize_mx(out=z_codes[:].bitcast(FP8X4), scales=z_plane[:], in_=z_bf16[c][:].rearrange("p v s -> p (v s)"))
             out_sums = psum.tile([P, pairs], F32, name=f"out_sums{c}", tag=f"bank{FIRST_OUT_BANK + c}")
             nc.tensor.matmul_mx(
                 out=out_sums[:],
@@ -202,24 +210,41 @@ def tile_picked_phpair_relu_p_kernel(tc, x_words, x_scales, w1, w2_words, w2_sca
                 stop=True,
             )
             result = keep.tile([P, pairs], F32, name=f"result{c}")
-            if last:
+            if on_vector:
                 nc.vector.tensor_copy(result[:], out_sums[:])
             else:
                 nc.scalar.copy(result[:], out_sums[:])
             nc.sync.dma_start(out[:, v0:v1], result[:])
 
-        early_diff = keep.tile([P, PACK, EARLY], F32, name="early_diff")
-        late_right = []
+        early_tags = ("w1_codes10", "early_right1", "w1_codes11", "early_right3")
+        early_right = []
         for s in range(PACK):
-            early_right = fetch_right(s, 0, EARLY, f"early_right{s}")
-            late_right.append(fetch_right(s, EARLY, V, f"late_right{s}"))
-            subtract(early_diff[:, s, :], s, 0, EARLY, early_right[:])
-        for c in range(2):
-            v0, v1 = PAIR_CHUNKS[c]
-            second_layer(early_diff[:, :, v0:v1], c)
-        for c, tag in ((2, f"early_right{PACK - 1}"), (3, "z_bf16_0")):
-            v0, v1 = PAIR_CHUNKS[c]
-            late_diff = keep.tile([P, PACK, v1 - v0], F32, name=f"late_diff{c}", tag=tag, align_bytes=64)
-            for s in range(PACK):
-                subtract(late_diff[:, s, :], s, v0, v1, late_right[s][:, v0 - EARLY : v1 - EARLY])
-            second_layer(late_diff[:], c)
+            multiply(s)
+            for u in range(len(sums[s])):
+                empty(s, u, on_vector=(u % 2 == 1))
+        for s in range(PACK):
+            early_right.append(keep.tile([P, HALF], F32, name=f"early_right{s}", tag=early_tags[s], align_bytes=64))
+            fetch_right(early_right[s][:], s, 0, HALF)
+            subtract(s, 0, HALF, early_right[s][:])
+        late_right = keep.tile([P, PACK, HALF], F32, name="late_right", tag="w1_bf16_00", align_bytes=64)
+        for s in range(PACK):
+            fetch_right(late_right[:, s, :], s, HALF, V)
+
+        def subtract_late(s, v0, v1):
+            subtract(s, v0, v1, late_right[:, s, v0 - HALF : v1 - HALF])
+
+        subtract_late(0, HALF, V)
+        rectify(0, 0, 128, on_vector=True)
+        rectify(1, 128, 256, on_vector=False)
+        subtract_late(1, HALF, V)
+        second_product(0, on_vector=False)
+        subtract_late(2, 256, 384)
+        subtract_late(3, 256, 384)
+        rectify(2, 256, 384, on_vector=False)
+        subtract_late(2, 384, V)
+        second_product(1, on_vector=False)
+        subtract_late(3, 384, V)
+        second_product(2, on_vector=False)
+        rectify(3, 384, 448, on_vector=True)
+        rectify(3, 448, V, on_vector=False)
+        second_product(3, on_vector=True)

@@ -27,11 +27,12 @@ PASS_ROW = 8
 FIRST_TOKENS = 3 * T // 8
 
 HALF = V // 2
-PAIR_CHUNKS = ((0, 128), (128, 256), (256, 384), (384, V))
+PAIR_CHUNKS = ((0, 128), (128, 256), (256, 384), (384, 448), (448, V))
+STORES = ((0, 256), (256, 448), (448, V))
 
 PLACES_PER_BANK = (BANK // 2, BANK, BANK, BANK)
-FIRST_BANK = (0, 4, 6, 0)
-FIRST_OUT_BANK = 2
+FIRST_BANK = (0, 4, 0, 2)
+FIRST_OUT_BANK = 4
 
 
 def tile_picked_phpair_relu_p_kernel(tc, x_words, x_scales, w1, w2_words, w2_scales, offs, left, right, out):
@@ -67,9 +68,10 @@ def tile_picked_phpair_relu_p_kernel(tc, x_words, x_scales, w1, w2_words, w2_sca
         nc.sync.dma_start(w1_first[:], w1_rows[0])
         load_words(1, 0, T)
 
-        w1_second_bytes = 4 * PACK * H
-        w1_second = placed.tile([P, 2, PACK, H // 2], F32, name="w1_second", align_bytes=64, offset=0)
-        picked_scales = placed.tile([P, S], U8, name="picked_scales", align_bytes=64, offset=w1_second_bytes - S // 4)
+        half_bytes = 4 * PACK * (H // 2)
+        w1_low = placed.tile([P, PACK, H // 2], F32, name="w1_low", align_bytes=64, offset=0)
+        picked_scales = placed.tile([P, S], U8, name="picked_scales", align_bytes=64, offset=half_bytes - 64)
+        w1_high = placed.tile([P, PACK, H // 2], F32, name="w1_high", align_bytes=64, offset=half_bytes + 5 * N)
         x_plane = keep.tile([P, S], U8, name="x_plane", align_bytes=64)
         nc.vector.tensor_copy(picked_scales[:], scale_table[:].indirect(offs_sb[:]))
         nc.vector.tensor_copy(x_plane[:].bitcast(I32), picked_scales[:].bitcast(I32))
@@ -79,11 +81,11 @@ def tile_picked_phpair_relu_p_kernel(tc, x_words, x_scales, w1, w2_words, w2_sca
                     x_plane[PASS_ROW * g + 2 + j : P : QUADRANT, :].bitcast(I32),
                     x_plane[GROUP + PASS_ROW * g + j : P : QUADRANT, :].bitcast(I32),
                 )
-        for u in range(2):
-            nc.sync.dma_start(w1_second[:, u, :, :], w1_rows[1][:, :, u * (H // 2) : (u + 1) * (H // 2)])
+        nc.sync.dma_start(w1_low[:], w1_rows[1][:, :, 0 : H // 2])
+        nc.sync.dma_start(w1_high[:], w1_rows[1][:, :, H // 2 : H])
 
-        w2_plane = placed.tile([P, N], U8, name="w2_plane", align_bytes=64, offset=w1_second_bytes)
-        w2_codes = placed.tile([P, N], I32, name="w2_codes", align_bytes=64, offset=w1_second_bytes + N)
+        w2_plane = placed.tile([P, N], U8, name="w2_plane", align_bytes=64, offset=half_bytes)
+        w2_codes = placed.tile([P, N], I32, name="w2_codes", align_bytes=64, offset=half_bytes + N)
         nc.gpsimd.memset(w2_plane[:].bitcast(I32), 0)
         nc.sync.dma_start(w2_codes[:], w2_words[0].rearrange("p n t -> p (n t)").bitcast(I32))
         for q in range(P // QUADRANT):
@@ -132,14 +134,15 @@ def tile_picked_phpair_relu_p_kernel(tc, x_words, x_scales, w1, w2_words, w2_sca
         quantize_w1(0, 0, 0, 2)
         pick_words(1, "w1_bf16_00")
         for d in range(2):
-            deal_on_scalar(1, d, w1_second[:, 0, :, :], 0, P // 2)
-        deal_on_vector(1, 0, w1_second[:, 1, :, :], P // 2, P)
-        deal_on_scalar(1, 1, w1_second[:, 1, :, :], P // 2, P)
+            deal_on_scalar(1, d, w1_low[:], 0, P // 2)
+        deal_on_vector(1, 0, w1_high[:, :, 0 : H // 4], P // 2, 3 * P // 4)
+        deal_on_scalar(1, 0, w1_high[:, :, H // 4 : H // 2], 3 * P // 4, P)
+        deal_on_scalar(1, 1, w1_high[:], P // 2, P)
+        w1_codes[0][1] = placed.tile([P, 2 * P], U32, name="w1_codes01", align_bytes=64, offset=0)
+        quantize_w1(0, 1, 0, 2)
         open_w1_codes(1, 0, "w1_codes10")
         quantize_w1(1, 0, 0, 1)
         quantize_w1(1, 0, 1, 2)
-        open_w1_codes(0, 1, "w1_bf16_10")
-        quantize_w1(0, 1, 0, 2)
         open_w1_codes(1, 1, "w1_codes11")
         quantize_w1(1, 1, 0, 2)
 
@@ -193,15 +196,15 @@ def tile_picked_phpair_relu_p_kernel(tc, x_words, x_scales, w1, w2_words, w2_sca
             else:
                 nc.scalar.activation(dst, src, ACT.Relu)
 
-        def second_product(c, on_vector):
+        out_sums = [psum.tile([P, v1 - v0], F32, name=f"out_sums{b}", tag=f"bank{FIRST_OUT_BANK + b}") for b, (v0, v1) in enumerate(STORES)]
+
+        def second_product(c, b):
             v0, v1 = PAIR_CHUNKS[c]
-            pairs = v1 - v0
-            z_codes = keep.tile([P, pairs], U32, name=f"z_codes{c}", align_bytes=64)
-            z_plane = keep.tile([P, pairs], U8, name=f"z_plane{c}", align_bytes=64)
+            z_codes = keep.tile([P, v1 - v0], U32, name=f"z_codes{c}", align_bytes=64)
+            z_plane = keep.tile([P, v1 - v0], U8, name=f"z_plane{c}", align_bytes=64)
             nc.vector.quantize_mx(out=z_codes[:].bitcast(FP8X4), scales=z_plane[:], in_=z_bf16[c][:].rearrange("p v s -> p (v s)"))
-            out_sums = psum.tile([P, pairs], F32, name=f"out_sums{c}", tag=f"bank{FIRST_OUT_BANK + c}")
             nc.tensor.matmul_mx(
-                out=out_sums[:],
+                out=out_sums[b][:, v0 - STORES[b][0] : v1 - STORES[b][0]],
                 lhsT=w2_codes[:].bitcast(FP8X4),
                 lhsT_scale=w2_plane[:],
                 rhs=z_codes[:].bitcast(FP8X4),
@@ -209,11 +212,14 @@ def tile_picked_phpair_relu_p_kernel(tc, x_words, x_scales, w1, w2_words, w2_sca
                 start=True,
                 stop=True,
             )
-            result = keep.tile([P, pairs], F32, name=f"result{c}")
+
+        def store(b, tag, on_vector):
+            v0, v1 = STORES[b]
+            result = keep.tile([P, v1 - v0], F32, name=f"result{b}", tag=tag, align_bytes=64)
             if on_vector:
-                nc.vector.tensor_copy(result[:], out_sums[:])
+                nc.vector.tensor_copy(result[:], out_sums[b][:])
             else:
-                nc.scalar.copy(result[:], out_sums[:])
+                nc.scalar.copy(result[:], out_sums[b][:])
             nc.sync.dma_start(out[:, v0:v1], result[:])
 
         early_tags = ("w1_codes10", "early_right1", "w1_codes11", "early_right3")
@@ -237,14 +243,19 @@ def tile_picked_phpair_relu_p_kernel(tc, x_words, x_scales, w1, w2_words, w2_sca
         rectify(0, 0, 128, on_vector=True)
         rectify(1, 128, 256, on_vector=False)
         subtract_late(1, HALF, V)
-        second_product(0, on_vector=False)
+        second_product(0, 0)
         subtract_late(2, 256, 384)
         subtract_late(3, 256, 384)
         rectify(2, 256, 384, on_vector=False)
         subtract_late(2, 384, V)
-        second_product(1, on_vector=False)
-        subtract_late(3, 384, V)
-        second_product(2, on_vector=False)
+        second_product(1, 0)
+        subtract_late(3, 384, 448)
+        subtract_late(3, 448, V)
         rectify(3, 384, 448, on_vector=True)
-        rectify(3, 448, V, on_vector=False)
-        second_product(3, on_vector=True)
+        rectify(4, 448, V, on_vector=False)
+        second_product(2, 1)
+        second_product(3, 1)
+        second_product(4, 2)
+        store(0, "w1_bf16_00", on_vector=False)
+        store(1, "result1", on_vector=False)
+        store(2, "result2", on_vector=True)

@@ -21,7 +21,7 @@ PASSES = K // (P * PACK)
 BANK = 512
 GROUP = 16
 QUADRANT = 32
-LINE = 2
+LINE = 4
 PASS_ROW = 8
 
 FIRST_TOKENS = 3 * T // 8

@@ -26,12 +26,12 @@ PASS_ROW = 8
 
 FIRST_TOKENS = 3 * T // 8
 
-HALF = V // 2
-PAIR_CHUNKS = ((0, 128), (128, 256), (256, 384), (384, 448), (448, V))
-STORES = ((0, 256), (256, 448), (448, V))
+STRETCHES = ((0, 256), (256, 768), (768, S))
+BANKS = ((0, 4, 6), (1, 5, 7), (2, 0, 1), (3, 2, 3))
 
-PLACES_PER_BANK = (BANK // 2, BANK, BANK, BANK)
-FIRST_BANK = (0, 4, 0, 2)
+HALF = V // 2
+PAIR_CHUNKS = ((0, 256), (256, 384), (384, V))
+SHARES = ((0, 128), (128, 256), (256, 384), (384, 448), (448, V))
 FIRST_OUT_BANK = 4
 
 
@@ -47,31 +47,33 @@ def tile_picked_phpair_relu_p_kernel(tc, x_words, x_scales, w1, w2_words, w2_sca
         left_sb = lists.tile([P, V // GROUP], U16, name="left_sb")
         right_sb = lists.tile([P, V // GROUP], U16, name="right_sb")
 
+        def entries(list_sb, j0, j1):
+            return list_sb[:, j0 // GROUP : j1 // GROUP]
+
         scale_table = keep.tile([P, T], U8, name="scale_table", align_bytes=64)
         nc.gpsimd.memset(scale_table[:].bitcast(I32), 0)
 
-        word_table = [keep.tile([P, T], I32, name=f"word_table{g}", align_bytes=64) for g in range(PASSES)]
+        def load_words(table, g, c0, c1):
+            nc.sync.dma_start(table[:, c0:c1], x_words[g].rearrange("p n t -> p (n t)").bitcast(I32)[:, c0:c1])
+
+        first_table = keep.tile([P, T], I32, name="first_table", align_bytes=64)
         w1_rows = w1.rearrange("(g p t) c -> g p t c", g=PASSES, t=PACK)
-        w1_first = keep.tile([P, PACK, H], F32, name="w1_first")
+        w1_raw = [keep.tile([P, PACK, H], F32, name=f"w1_raw{g}") for g in range(PASSES)]
 
-        def load_words(g, c0, c1):
-            nc.sync.dma_start(word_table[g][:, c0:c1], x_words[g].rearrange("p n t -> p (n t)").bitcast(I32)[:, c0:c1])
-
-        load_words(0, 0, FIRST_TOKENS)
+        load_words(first_table, 0, 0, FIRST_TOKENS)
         nc.sync.dma_start(offs_sb[:], offs)
         nc.sync.dma_start(left_sb[:], left)
         nc.sync.dma_start(right_sb[:], right)
         scale_rows = x_scales.bitcast(I32).rearrange("g (r j) c -> j r g c", j=2)
         for j in range(2):
             nc.sync.dma_start(scale_table[j:P:PASS_ROW, :].bitcast(I32), scale_rows[j])
-        load_words(0, FIRST_TOKENS, T)
-        nc.sync.dma_start(w1_first[:], w1_rows[0])
-        load_words(1, 0, T)
+        load_words(first_table, 0, FIRST_TOKENS, T)
+        for g in range(PASSES):
+            nc.sync.dma_start(w1_raw[g][:], w1_rows[g])
 
-        half_bytes = 4 * PACK * (H // 2)
-        w1_low = placed.tile([P, PACK, H // 2], F32, name="w1_low", align_bytes=64, offset=0)
-        picked_scales = placed.tile([P, S], U8, name="picked_scales", align_bytes=64, offset=half_bytes - 64)
-        w1_high = placed.tile([P, PACK, H // 2], F32, name="w1_high", align_bytes=64, offset=half_bytes + 5 * N)
+        table_bytes = 4 * T
+        last_table = placed.tile([P, T], I32, name="last_table", align_bytes=64, offset=0)
+        picked_scales = placed.tile([P, S], U8, name="picked_scales", align_bytes=64, offset=table_bytes - 64)
         x_plane = keep.tile([P, S], U8, name="x_plane", align_bytes=64)
         nc.vector.tensor_copy(picked_scales[:], scale_table[:].indirect(offs_sb[:]))
         nc.vector.tensor_copy(x_plane[:].bitcast(I32), picked_scales[:].bitcast(I32))
@@ -81,11 +83,10 @@ def tile_picked_phpair_relu_p_kernel(tc, x_words, x_scales, w1, w2_words, w2_sca
                     x_plane[PASS_ROW * g + 2 + j : P : QUADRANT, :].bitcast(I32),
                     x_plane[GROUP + PASS_ROW * g + j : P : QUADRANT, :].bitcast(I32),
                 )
-        nc.sync.dma_start(w1_low[:], w1_rows[1][:, :, 0 : H // 2])
-        nc.sync.dma_start(w1_high[:], w1_rows[1][:, :, H // 2 : H])
+        load_words(last_table, 1, 0, T)
 
-        w2_plane = placed.tile([P, N], U8, name="w2_plane", align_bytes=64, offset=half_bytes)
-        w2_codes = placed.tile([P, N], I32, name="w2_codes", align_bytes=64, offset=half_bytes + N)
+        w2_plane = placed.tile([P, N], U8, name="w2_plane", align_bytes=64, offset=table_bytes)
+        w2_codes = placed.tile([P, N], I32, name="w2_codes", align_bytes=64, offset=table_bytes + N)
         nc.gpsimd.memset(w2_plane[:].bitcast(I32), 0)
         nc.sync.dma_start(w2_codes[:], w2_words[0].rearrange("p n t -> p (n t)").bitcast(I32))
         for q in range(P // QUADRANT):
@@ -94,100 +95,85 @@ def tile_picked_phpair_relu_p_kernel(tc, x_words, x_scales, w1, w2_words, w2_sca
                 w2_scales[0].bitcast(I32)[4 * q : 4 * q + 4, :],
             )
 
-        x_codes = [None] * PASSES
+        x_codes = [keep.tile([P, S], U32, name=f"x_codes{g}", align_bytes=64) for g in range(PASSES)]
+        nc.vector.tensor_copy(x_codes[0][:], first_table[:].bitcast(U32).indirect(offs_sb[:]))
 
-        def pick_words(g, tag):
-            x_codes[g] = keep.tile([P, S], U32, name=f"x_codes{g}", tag=tag, align_bytes=64)
-            nc.vector.tensor_copy(x_codes[g][:], word_table[g][:].bitcast(U32).indirect(offs_sb[:]))
-
-        w1_bf16 = [[keep.tile([P, 2, P, PACK], BF16, name=f"w1_bf16_{g}{d}", align_bytes=64) for d in range(2)] for g in range(PASSES)]
-        w1_codes = [[None] * 2 for g in range(PASSES)]
+        tags = (("a", "b"), ("c", "a"))
+        w1_bf16 = [[keep.tile([P, 2, P, PACK], BF16, name=f"w1_bf16_{g}{d}", tag=f"w1_bf16_{tags[g][d]}", align_bytes=64) for d in range(2)] for g in range(PASSES)]
+        w1_codes = [[keep.tile([P, 2 * P], U32, name=f"w1_codes{g}{d}", align_bytes=64) for d in range(2)] for g in range(PASSES)]
         w1_plane = [[keep.tile([P, 2 * P], U8, name=f"w1_plane{g}{d}", align_bytes=64) for d in range(2)] for g in range(PASSES)]
 
-        def deal_views(g, d, raw, m0, m1):
-            dst = w1_bf16[g][d][:, :, m0:m1, :].rearrange("p e m t -> p m t e")
-            src = raw.rearrange("p t (m s) -> p m t s", s=PACK)[:, :, :, 2 * d : 2 * d + 2]
-            return dst, src
+        def deal(g, d, on_vector):
+            dst = w1_bf16[g][d][:].rearrange("p e m t -> p m t e")
+            src = w1_raw[g][:].rearrange("p t (m s) -> p m t s", s=PACK)[:, :, :, 2 * d : 2 * d + 2]
+            if on_vector:
+                nc.vector.tensor_copy(dst, src)
+            else:
+                nc.scalar.copy(dst, src)
 
-        def deal_on_scalar(g, d, raw, m0, m1):
-            dst, src = deal_views(g, d, raw, m0, m1)
-            nc.scalar.copy(dst, src)
-
-        def deal_on_vector(g, d, raw, m0, m1):
-            dst, src = deal_views(g, d, raw, m0, m1)
-            nc.vector.tensor_copy(dst, src)
-
-        def open_w1_codes(g, d, tag):
-            w1_codes[g][d] = keep.tile([P, 2 * P], U32, name=f"w1_codes{g}{d}", tag=tag, align_bytes=64)
-
-        def quantize_w1(g, d, e0, e1):
+        def quantize_w1(g, d):
             nc.vector.quantize_mx(
-                out=w1_codes[g][d][:, e0 * P : e1 * P].bitcast(FP8X4),
-                scales=w1_plane[g][d][:, e0 * P : e1 * P],
-                in_=w1_bf16[g][d][:, e0:e1, :, :].rearrange("p e m t -> p (e m t)"),
+                out=w1_codes[g][d][:].bitcast(FP8X4),
+                scales=w1_plane[g][d][:],
+                in_=w1_bf16[g][d][:].rearrange("p e m t -> p (e m t)"),
             )
 
-        pick_words(0, "x_codes0")
         for d in range(2):
-            deal_on_scalar(0, d, w1_first[:], 0, P)
-        open_w1_codes(0, 0, "w1_codes00")
-        quantize_w1(0, 0, 0, 2)
-        pick_words(1, "w1_bf16_00")
+            deal(0, d, on_vector=False)
+            quantize_w1(0, d)
+        deal(1, 0, on_vector=False)
+        deal(1, 1, on_vector=True)
         for d in range(2):
-            deal_on_scalar(1, d, w1_low[:], 0, P // 2)
-        deal_on_vector(1, 0, w1_high[:, :, 0 : H // 4], P // 2, 3 * P // 4)
-        deal_on_scalar(1, 0, w1_high[:, :, H // 4 : H // 2], 3 * P // 4, P)
-        deal_on_scalar(1, 1, w1_high[:], P // 2, P)
-        w1_codes[0][1] = placed.tile([P, 2 * P], U32, name="w1_codes01", align_bytes=64, offset=0)
-        quantize_w1(0, 1, 0, 2)
-        open_w1_codes(1, 0, "w1_codes10")
-        quantize_w1(1, 0, 0, 1)
-        quantize_w1(1, 0, 1, 2)
-        open_w1_codes(1, 1, "w1_codes11")
-        quantize_w1(1, 1, 0, 2)
+            quantize_w1(1, d)
+        for j0, j1 in STRETCHES:
+            nc.vector.tensor_copy(x_codes[1][:, j0:j1], last_table[:].bitcast(U32).indirect(entries(offs_sb, j0, j1)))
 
         h = [keep.tile([P, S], F32, name=f"h{s}") for s in range(PACK)]
-        sums = [None] * PACK
+        sums = [[None] * len(STRETCHES) for s in range(PACK)]
 
-        def multiply(s):
-            width = PLACES_PER_BANK[s]
-            sums[s] = [psum.tile([P, width], F32, name=f"sums{s}{u}", tag=f"bank{FIRST_BANK[s] + u}") for u in range(S // width)]
+        def multiply(s, u, g):
+            places = slice(*STRETCHES[u])
+            if g == 0:
+                sums[s][u] = psum.tile([P, places.stop - places.start], F32, name=f"sums{s}{u}", tag=f"bank{BANKS[s][u]}")
             d, columns = s // 2, slice((s % 2) * P, (s % 2 + 1) * P)
-            for g in range(PASSES):
-                for u, bank in enumerate(sums[s]):
-                    places = slice(u * width, (u + 1) * width)
-                    nc.tensor.matmul_mx(
-                        out=bank[:],
-                        lhsT=w1_codes[g][d][:, columns].bitcast(FP8X4),
-                        lhsT_scale=w1_plane[g][d][:, columns],
-                        rhs=x_codes[g][:, places].bitcast(FP8X4),
-                        rhs_scale=x_plane[PASS_ROW * g : P, places],
-                        start=(g == 0),
-                        stop=(g == PASSES - 1),
-                    )
+            nc.tensor.matmul_mx(
+                out=sums[s][u][:],
+                lhsT=w1_codes[g][d][:, columns].bitcast(FP8X4),
+                lhsT_scale=w1_plane[g][d][:, columns],
+                rhs=x_codes[g][:, places].bitcast(FP8X4),
+                rhs_scale=x_plane[PASS_ROW * g : P, places],
+                start=(g == 0),
+                stop=(g == PASSES - 1),
+            )
 
         def empty(s, u, on_vector):
-            width = PLACES_PER_BANK[s]
+            places = slice(*STRETCHES[u])
             if on_vector:
-                nc.vector.tensor_copy(h[s][:, u * width : (u + 1) * width], sums[s][u][:])
+                nc.vector.tensor_copy(h[s][:, places], sums[s][u][:])
             else:
-                nc.scalar.copy(h[s][:, u * width : (u + 1) * width], sums[s][u][:])
+                nc.scalar.copy(h[s][:, places], sums[s][u][:])
 
-        def entries(list_sb, v0, v1):
-            return list_sb[:, v0 // GROUP : v1 // GROUP]
+        h_right = [[None] * 2 for s in range(PACK)]
 
-        def fetch_right(dst, s, v0, v1):
-            nc.scalar.activation(dst, h[s][:].indirect(entries(right_sb, v0, v1)), ACT.Copy)
+        def fetch_right(s, a, tag, on_vector):
+            h_right[s][a] = keep.tile([P, HALF], F32, name=f"h_right{s}{a}", tag=tag, align_bytes=64)
+            window = h[s][:].indirect(entries(right_sb, a * HALF, (a + 1) * HALF))
+            if on_vector:
+                nc.vector.tensor_copy(h_right[s][a][:], window)
+            else:
+                nc.scalar.activation(h_right[s][a][:], window, ACT.Copy)
 
         diff = [keep.tile([P, PACK, HALF], F32, name=f"diff{a}", align_bytes=64) for a in range(2)]
 
-        def subtract(s, v0, v1, h_right):
+        def subtract(s, v0, v1):
             a = v0 // HALF
-            nc.vector.tensor_tensor(diff[a][:, s, v0 - a * HALF : v1 - a * HALF], h[s][:].indirect(entries(left_sb, v0, v1)), h_right, ALU.subtract)
+            pairs = slice(v0 - a * HALF, v1 - a * HALF)
+            nc.vector.tensor_tensor(diff[a][:, s, pairs], h[s][:].indirect(entries(left_sb, v0, v1)), h_right[s][a][:, pairs], ALU.subtract)
 
         z_bf16 = [keep.tile([P, v1 - v0, PACK], BF16, name=f"z_bf16_{c}", align_bytes=64) for c, (v0, v1) in enumerate(PAIR_CHUNKS)]
 
-        def rectify(c, v0, v1, on_vector):
+        def rectify(c, share, on_vector):
+            v0, v1 = SHARES[share]
             a, first = v0 // HALF, PAIR_CHUNKS[c][0]
             dst = z_bf16[c][:, v0 - first : v1 - first, :].rearrange("p (a b) s -> p a s b", b=LINE)
             src = diff[a][:, :, v0 - a * HALF : v1 - a * HALF].rearrange("p s (a b) -> p a s b", b=LINE)
@@ -196,7 +182,7 @@ def tile_picked_phpair_relu_p_kernel(tc, x_words, x_scales, w1, w2_words, w2_sca
             else:
                 nc.scalar.activation(dst, src, ACT.Relu)
 
-        out_sums = [psum.tile([P, v1 - v0], F32, name=f"out_sums{b}", tag=f"bank{FIRST_OUT_BANK + b}") for b, (v0, v1) in enumerate(STORES)]
+        out_sums = [psum.tile([P, v1 - v0], F32, name=f"out_sums{b}", tag=f"bank{FIRST_OUT_BANK + b}") for b, (v0, v1) in enumerate(PAIR_CHUNKS)]
 
         def second_product(c, b):
             v0, v1 = PAIR_CHUNKS[c]
@@ -204,7 +190,7 @@ def tile_picked_phpair_relu_p_kernel(tc, x_words, x_scales, w1, w2_words, w2_sca
             z_plane = keep.tile([P, v1 - v0], U8, name=f"z_plane{c}", align_bytes=64)
             nc.vector.quantize_mx(out=z_codes[:].bitcast(FP8X4), scales=z_plane[:], in_=z_bf16[c][:].rearrange("p v s -> p (v s)"))
             nc.tensor.matmul_mx(
-                out=out_sums[b][:, v0 - STORES[b][0] : v1 - STORES[b][0]],
+                out=out_sums[b][:, v0 - PAIR_CHUNKS[b][0] : v1 - PAIR_CHUNKS[b][0]],
                 lhsT=w2_codes[:].bitcast(FP8X4),
                 lhsT_scale=w2_plane[:],
                 rhs=z_codes[:].bitcast(FP8X4),
@@ -214,7 +200,7 @@ def tile_picked_phpair_relu_p_kernel(tc, x_words, x_scales, w1, w2_words, w2_sca
             )
 
         def store(b, tag, on_vector):
-            v0, v1 = STORES[b]
+            v0, v1 = PAIR_CHUNKS[b]
             result = keep.tile([P, v1 - v0], F32, name=f"result{b}", tag=tag, align_bytes=64)
             if on_vector:
                 nc.vector.tensor_copy(result[:], out_sums[b][:])
@@ -222,40 +208,50 @@ def tile_picked_phpair_relu_p_kernel(tc, x_words, x_scales, w1, w2_words, w2_sca
                 nc.scalar.copy(result[:], out_sums[b][:])
             nc.sync.dma_start(out[:, v0:v1], result[:])
 
-        early_tags = ("w1_codes10", "early_right1", "w1_codes11", "early_right3")
-        early_right = []
         for s in range(PACK):
-            multiply(s)
-            for u in range(len(sums[s])):
-                empty(s, u, on_vector=(u % 2 == 1))
+            multiply(s, 0, 0)
+        for s in range(2):
+            for u in (1, 2):
+                multiply(s, u, 0)
         for s in range(PACK):
-            early_right.append(keep.tile([P, HALF], F32, name=f"early_right{s}", tag=early_tags[s], align_bytes=64))
-            fetch_right(early_right[s][:], s, 0, HALF)
-            subtract(s, 0, HALF, early_right[s][:])
-        late_right = keep.tile([P, PACK, HALF], F32, name="late_right", tag="w1_bf16_00", align_bytes=64)
-        for s in range(PACK):
-            fetch_right(late_right[:, s, :], s, HALF, V)
-
-        def subtract_late(s, v0, v1):
-            subtract(s, v0, v1, late_right[:, s, v0 - HALF : v1 - HALF])
-
-        subtract_late(0, HALF, V)
-        rectify(0, 0, 128, on_vector=True)
-        rectify(1, 128, 256, on_vector=False)
-        subtract_late(1, HALF, V)
+            multiply(s, 0, 1)
+            empty(s, 0, on_vector=(s == 3))
+        for u in (1, 2):
+            for s in range(2):
+                multiply(s, u, 1)
+                empty(s, u, on_vector=(s, u) == (1, 1))
+        for s in range(2, PACK):
+            for u in (1, 2):
+                for g in range(PASSES):
+                    multiply(s, u, g)
+                empty(s, u, on_vector=False)
+            if s == 2:
+                fetch_right(1, 0, "h_right10", on_vector=False)
+        for a in range(2):
+            fetch_right(0, a, f"h_right0{a}", on_vector=True)
+        for a in range(2):
+            subtract(0, a * HALF, (a + 1) * HALF)
+        fetch_right(1, 1, "h_right11", on_vector=False)
+        fetch_right(2, 0, "h_right20", on_vector=False)
+        fetch_right(3, 0, "h_right30", on_vector=False)
+        fetch_right(2, 1, "h_right21", on_vector=False)
+        fetch_right(3, 1, "h_right31", on_vector=False)
+        subtract(1, 0, HALF)
+        subtract(1, HALF, V)
+        subtract(2, 0, HALF)
+        subtract(3, 0, HALF)
+        subtract(2, HALF, V)
+        rectify(0, 0, on_vector=False)
+        subtract(3, 256, 384)
+        rectify(1, 2, on_vector=False)
+        rectify(0, 1, on_vector=True)
+        subtract(3, 384, 448)
+        rectify(2, 3, on_vector=False)
+        subtract(3, 448, V)
         second_product(0, 0)
-        subtract_late(2, 256, 384)
-        subtract_late(3, 256, 384)
-        rectify(2, 256, 384, on_vector=False)
-        subtract_late(2, 384, V)
-        second_product(1, 0)
-        subtract_late(3, 384, 448)
-        subtract_late(3, 448, V)
-        rectify(3, 384, 448, on_vector=True)
-        rectify(4, 448, V, on_vector=False)
-        second_product(2, 1)
-        second_product(3, 1)
-        second_product(4, 2)
-        store(0, "w1_bf16_00", on_vector=False)
+        rectify(2, 4, on_vector=True)
+        second_product(1, 1)
+        second_product(2, 2)
+        store(0, "result0", on_vector=False)
         store(1, "result1", on_vector=False)
         store(2, "result2", on_vector=True)

@@ -30,8 +30,8 @@ STRETCHES = ((0, 256), (256, 768), (768, S))
 BANKS = ((0, 4, 6), (1, 5, 7), (2, 0, 1), (3, 2, 3))
 
 HALF = V // 2
-PAIR_CHUNKS = ((0, 256), (256, 384), (384, V))
-SHARES = ((0, 128), (128, 256), (256, 384), (384, 448), (448, V))
+PAIR_CHUNKS = ((0, 256), (256, 384), (384, 448), (448, V))
+STORES = ((0, 256), (256, 448), (448, V))
 FIRST_OUT_BANK = 4
 
 
@@ -153,36 +153,31 @@ def tile_picked_phpair_relu_p_kernel(tc, x_words, x_scales, w1, w2_words, w2_sca
             else:
                 nc.scalar.copy(h[s][:, places], sums[s][u][:])
 
-        h_right = [[None] * 2 for s in range(PACK)]
+        h_right = [keep.tile([P, V], F32, name=f"h_right{s}", align_bytes=64) for s in range(PACK)]
+        diff = keep.tile([P, PACK, V], F32, name="diff", align_bytes=64)
 
-        def fetch_right(s, a, tag, on_vector):
-            h_right[s][a] = keep.tile([P, HALF], F32, name=f"h_right{s}{a}", tag=tag, align_bytes=64)
-            window = h[s][:].indirect(entries(right_sb, a * HALF, (a + 1) * HALF))
+        def fetch_right(s, v0, v1, on_vector):
+            window = h[s][:].indirect(entries(right_sb, v0, v1))
             if on_vector:
-                nc.vector.tensor_copy(h_right[s][a][:], window)
+                nc.vector.tensor_copy(h_right[s][:, v0:v1], window)
             else:
-                nc.scalar.activation(h_right[s][a][:], window, ACT.Copy)
-
-        diff = [keep.tile([P, PACK, HALF], F32, name=f"diff{a}", align_bytes=64) for a in range(2)]
+                nc.scalar.activation(h_right[s][:, v0:v1], window, ACT.Copy)
 
         def subtract(s, v0, v1):
-            a = v0 // HALF
-            pairs = slice(v0 - a * HALF, v1 - a * HALF)
-            nc.vector.tensor_tensor(diff[a][:, s, pairs], h[s][:].indirect(entries(left_sb, v0, v1)), h_right[s][a][:, pairs], ALU.subtract)
+            nc.vector.tensor_tensor(diff[:, s, v0:v1], h[s][:].indirect(entries(left_sb, v0, v1)), h_right[s][:, v0:v1], ALU.subtract)
 
         z_bf16 = [keep.tile([P, v1 - v0, PACK], BF16, name=f"z_bf16_{c}", align_bytes=64) for c, (v0, v1) in enumerate(PAIR_CHUNKS)]
 
-        def rectify(c, share, on_vector):
-            v0, v1 = SHARES[share]
-            a, first = v0 // HALF, PAIR_CHUNKS[c][0]
+        def rectify(c, v0, v1, on_vector):
+            first = PAIR_CHUNKS[c][0]
             dst = z_bf16[c][:, v0 - first : v1 - first, :].rearrange("p (a b) s -> p a s b", b=LINE)
-            src = diff[a][:, :, v0 - a * HALF : v1 - a * HALF].rearrange("p s (a b) -> p a s b", b=LINE)
+            src = diff[:, :, v0:v1].rearrange("p s (a b) -> p a s b", b=LINE)
             if on_vector:
                 nc.vector.tensor_scalar(dst, src, 0.0, None, ALU.max)
             else:
                 nc.scalar.activation(dst, src, ACT.Relu)
 
-        out_sums = [psum.tile([P, v1 - v0], F32, name=f"out_sums{b}", tag=f"bank{FIRST_OUT_BANK + b}") for b, (v0, v1) in enumerate(PAIR_CHUNKS)]
+        out_sums = [psum.tile([P, v1 - v0], F32, name=f"out_sums{b}", tag=f"bank{FIRST_OUT_BANK + b}") for b, (v0, v1) in enumerate(STORES)]
 
         def second_product(c, b):
             v0, v1 = PAIR_CHUNKS[c]
@@ -190,7 +185,7 @@ def tile_picked_phpair_relu_p_kernel(tc, x_words, x_scales, w1, w2_words, w2_sca
             z_plane = keep.tile([P, v1 - v0], U8, name=f"z_plane{c}", align_bytes=64)
             nc.vector.quantize_mx(out=z_codes[:].bitcast(FP8X4), scales=z_plane[:], in_=z_bf16[c][:].rearrange("p v s -> p (v s)"))
             nc.tensor.matmul_mx(
-                out=out_sums[b][:, v0 - PAIR_CHUNKS[b][0] : v1 - PAIR_CHUNKS[b][0]],
+                out=out_sums[b][:, v0 - STORES[b][0] : v1 - STORES[b][0]],
                 lhsT=w2_codes[:].bitcast(FP8X4),
                 lhsT_scale=w2_plane[:],
                 rhs=z_codes[:].bitcast(FP8X4),
@@ -200,7 +195,7 @@ def tile_picked_phpair_relu_p_kernel(tc, x_words, x_scales, w1, w2_words, w2_sca
             )
 
         def store(b, tag, on_vector):
-            v0, v1 = PAIR_CHUNKS[b]
+            v0, v1 = STORES[b]
             result = keep.tile([P, v1 - v0], F32, name=f"result{b}", tag=tag, align_bytes=64)
             if on_vector:
                 nc.vector.tensor_copy(result[:], out_sums[b][:])
@@ -215,7 +210,7 @@ def tile_picked_phpair_relu_p_kernel(tc, x_words, x_scales, w1, w2_words, w2_sca
                 multiply(s, u, 0)
         for s in range(PACK):
             multiply(s, 0, 1)
-            empty(s, 0, on_vector=(s == 3))
+            empty(s, 0, on_vector=False)
         for u in (1, 2):
             for s in range(2):
                 multiply(s, u, 1)
@@ -224,34 +219,35 @@ def tile_picked_phpair_relu_p_kernel(tc, x_words, x_scales, w1, w2_words, w2_sca
             for u in (1, 2):
                 for g in range(PASSES):
                     multiply(s, u, g)
-                empty(s, u, on_vector=False)
-            if s == 2:
-                fetch_right(1, 0, "h_right10", on_vector=False)
-        for a in range(2):
-            fetch_right(0, a, f"h_right0{a}", on_vector=True)
-        for a in range(2):
-            subtract(0, a * HALF, (a + 1) * HALF)
-        fetch_right(1, 1, "h_right11", on_vector=False)
-        fetch_right(2, 0, "h_right20", on_vector=False)
-        fetch_right(3, 0, "h_right30", on_vector=False)
-        fetch_right(2, 1, "h_right21", on_vector=False)
-        fetch_right(3, 1, "h_right31", on_vector=False)
-        subtract(1, 0, HALF)
-        subtract(1, HALF, V)
+        empty(2, 1, on_vector=False)
+        fetch_right(1, 0, HALF, on_vector=False)
+        empty(2, 2, on_vector=False)
+        fetch_right(1, HALF, V, on_vector=False)
+        for u in (1, 2):
+            empty(3, u, on_vector=False)
+        for v0 in (0, HALF):
+            for s in (2, 3):
+                fetch_right(s, v0, v0 + HALF, on_vector=False)
+        for v0 in (0, HALF):
+            fetch_right(0, v0, v0 + HALF, on_vector=True)
+        for s in range(2):
+            for v0 in (0, HALF):
+                subtract(s, v0, v0 + HALF)
         subtract(2, 0, HALF)
         subtract(3, 0, HALF)
+        rectify(0, 0, 128, on_vector=False)
         subtract(2, HALF, V)
-        rectify(0, 0, on_vector=False)
         subtract(3, 256, 384)
-        rectify(1, 2, on_vector=False)
-        rectify(0, 1, on_vector=True)
+        rectify(1, 256, 384, on_vector=False)
+        rectify(0, 128, 256, on_vector=True)
         subtract(3, 384, 448)
-        rectify(2, 3, on_vector=False)
-        subtract(3, 448, V)
+        rectify(2, 384, 448, on_vector=False)
         second_product(0, 0)
-        rectify(2, 4, on_vector=True)
+        subtract(3, 448, V)
+        rectify(3, 448, V, on_vector=False)
         second_product(1, 1)
-        second_product(2, 2)
+        second_product(2, 1)
+        second_product(3, 2)
         store(0, "result0", on_vector=False)
         store(1, "result1", on_vector=False)
         store(2, "result2", on_vector=True)

@@ -103,9 +103,9 @@ def tile_picked_phpair_relu_p_kernel(tc, x_words, x_scales, w1, w2_words, w2_sca
         w1_codes = [[keep.tile([P, 2 * P], U32, name=f"w1_codes{g}{d}", align_bytes=64) for d in range(2)] for g in range(PASSES)]
         w1_plane = [[keep.tile([P, 2 * P], U8, name=f"w1_plane{g}{d}", align_bytes=64) for d in range(2)] for g in range(PASSES)]
 
-        def deal(g, d, on_vector):
-            dst = w1_bf16[g][d][:].rearrange("p e m t -> p m t e")
-            src = w1_raw[g][:].rearrange("p t (m s) -> p m t s", s=PACK)[:, :, :, 2 * d : 2 * d + 2]
+        def deal(g, d, m0, m1, on_vector):
+            dst = w1_bf16[g][d][:, :, m0:m1, :].rearrange("p e m t -> p m t e")
+            src = w1_raw[g][:].rearrange("p t (m s) -> p m t s", s=PACK)[:, m0:m1, :, 2 * d : 2 * d + 2]
             if on_vector:
                 nc.vector.tensor_copy(dst, src)
             else:
@@ -118,12 +118,14 @@ def tile_picked_phpair_relu_p_kernel(tc, x_words, x_scales, w1, w2_words, w2_sca
                 in_=w1_bf16[g][d][:].rearrange("p e m t -> p (e m t)"),
             )
 
+        deal(0, 0, 0, P, on_vector=False)
+        deal(0, 1, 0, P // 2, on_vector=False)
+        deal(0, 1, P // 2, P, on_vector=True)
         for d in range(2):
-            deal(0, d, on_vector=False)
             quantize_w1(0, d)
-        deal(1, 0, on_vector=False)
-        deal(1, 1, on_vector=True)
-        for d in range(2):
+        deal(1, 0, 0, P, on_vector=False)
+        deal(1, 1, 0, P, on_vector=True)
+        for d in (1, 0):
             quantize_w1(1, d)
         for j0, j1 in STRETCHES:
             nc.vector.tensor_copy(x_codes[1][:, j0:j1], last_table[:].bitcast(U32).indirect(entries(offs_sb, j0, j1)))
@@ -210,7 +212,7 @@ def tile_picked_phpair_relu_p_kernel(tc, x_words, x_scales, w1, w2_words, w2_sca
                 multiply(s, u, 0)
         for s in range(PACK):
             multiply(s, 0, 1)
-            empty(s, 0, on_vector=False)
+            empty(s, 0, on_vector=(s == 3))
         for u in (1, 2):
             for s in range(2):
                 multiply(s, u, 1)
@@ -220,9 +222,8 @@ def tile_picked_phpair_relu_p_kernel(tc, x_words, x_scales, w1, w2_words, w2_sca
                 for g in range(PASSES):
                     multiply(s, u, g)
         empty(2, 1, on_vector=False)
-        fetch_right(1, 0, HALF, on_vector=False)
+        fetch_right(1, 0, V, on_vector=False)
         empty(2, 2, on_vector=False)
-        fetch_right(1, HALF, V, on_vector=False)
         for u in (1, 2):
             empty(3, u, on_vector=False)
         for v0 in (0, HALF):
@@ -230,16 +231,16 @@ def tile_picked_phpair_relu_p_kernel(tc, x_words, x_scales, w1, w2_words, w2_sca
                 fetch_right(s, v0, v0 + HALF, on_vector=False)
         for v0 in (0, HALF):
             fetch_right(0, v0, v0 + HALF, on_vector=True)
-        for s in range(2):
-            for v0 in (0, HALF):
-                subtract(s, v0, v0 + HALF)
+        for v0 in (0, HALF):
+            subtract(0, v0, v0 + HALF)
+        subtract(1, 0, V)
         subtract(2, 0, HALF)
         subtract(3, 0, HALF)
-        rectify(0, 0, 128, on_vector=False)
+        rectify(0, 0, 192, on_vector=False)
         subtract(2, HALF, V)
         subtract(3, 256, 384)
         rectify(1, 256, 384, on_vector=False)
-        rectify(0, 128, 256, on_vector=True)
+        rectify(0, 192, 256, on_vector=True)
         subtract(3, 384, 448)
         rectify(2, 384, 448, on_vector=False)
         second_product(0, 0)

@@ -98,7 +98,7 @@ def tile_picked_phpair_relu_p_kernel(tc, x_words, x_scales, w1, w2_words, w2_sca
         x_codes = [keep.tile([P, S], U32, name=f"x_codes{g}", align_bytes=64) for g in range(PASSES)]
         nc.vector.tensor_copy(x_codes[0][:], first_table[:].bitcast(U32).indirect(offs_sb[:]))
 
-        tags = (("a", "b"), ("c", "a"))
+        tags = (("a", "b"), ("c", "b"))
         w1_bf16 = [[keep.tile([P, 2, P, PACK], BF16, name=f"w1_bf16_{g}{d}", tag=f"w1_bf16_{tags[g][d]}", align_bytes=64) for d in range(2)] for g in range(PASSES)]
         w1_codes = [[keep.tile([P, 2 * P], U32, name=f"w1_codes{g}{d}", align_bytes=64) for d in range(2)] for g in range(PASSES)]
         w1_plane = [[keep.tile([P, 2 * P], U8, name=f"w1_plane{g}{d}", align_bytes=64) for d in range(2)] for g in range(PASSES)]
@@ -118,14 +118,13 @@ def tile_picked_phpair_relu_p_kernel(tc, x_words, x_scales, w1, w2_words, w2_sca
                 in_=w1_bf16[g][d][:].rearrange("p e m t -> p (e m t)"),
             )
 
-        deal(0, 0, 0, P, on_vector=False)
-        deal(0, 1, 0, P // 2, on_vector=False)
-        deal(0, 1, P // 2, P, on_vector=True)
         for d in range(2):
+            deal(0, d, 0, P, on_vector=False)
             quantize_w1(0, d)
         deal(1, 0, 0, P, on_vector=False)
-        deal(1, 1, 0, P, on_vector=True)
-        for d in (1, 0):
+        deal(1, 1, 0, 3 * P // 4, on_vector=True)
+        deal(1, 1, 3 * P // 4, P, on_vector=False)
+        for d in range(2):
             quantize_w1(1, d)
         for j0, j1 in STRETCHES:
             nc.vector.tensor_copy(x_codes[1][:, j0:j1], last_table[:].bitcast(U32).indirect(entries(offs_sb, j0, j1)))

@@ -74,16 +74,21 @@ def tile_picked_phpair_relu_p_kernel(tc, x_words, x_scales, w1, w2_words, w2_sca
         table_bytes = 4 * T
         last_table = placed.tile([P, T], I32, name="last_table", align_bytes=64, offset=0)
         picked_scales = placed.tile([P, S], U8, name="picked_scales", align_bytes=64, offset=table_bytes - 64)
-        x_plane = keep.tile([P, S], U8, name="x_plane", align_bytes=64)
+        x_plane = [keep.tile([P, S], U8, name=f"x_plane{g}", align_bytes=64) for g in range(PASSES)]
         nc.vector.tensor_copy(picked_scales[:], scale_table[:].indirect(offs_sb[:]))
-        nc.vector.tensor_copy(x_plane[:].bitcast(I32), picked_scales[:].bitcast(I32))
         for g in range(PASSES):
+            nc.vector.tensor_copy(x_plane[g][:].bitcast(I32), picked_scales[:].bitcast(I32))
+
+        def move_odd_rows(g):
             for j in range(2):
                 nc.sync.dma_start(
-                    x_plane[PASS_ROW * g + 2 + j : P : QUADRANT, :].bitcast(I32),
-                    x_plane[GROUP + PASS_ROW * g + j : P : QUADRANT, :].bitcast(I32),
+                    x_plane[g][PASS_ROW * g + 2 + j : P : QUADRANT, :].bitcast(I32),
+                    x_plane[g][GROUP + PASS_ROW * g + j : P : QUADRANT, :].bitcast(I32),
                 )
+
+        move_odd_rows(0)
         load_words(last_table, 1, 0, T)
+        move_odd_rows(1)
 
         w2_plane = placed.tile([P, N], U8, name="w2_plane", align_bytes=64, offset=table_bytes)
         w2_codes = placed.tile([P, N], I32, name="w2_codes", align_bytes=64, offset=table_bytes + N)
@@ -142,7 +147,7 @@ def tile_picked_phpair_relu_p_kernel(tc, x_words, x_scales, w1, w2_words, w2_sca
                 lhsT=w1_codes[g][d][:, columns].bitcast(FP8X4),
                 lhsT_scale=w1_plane[g][d][:, columns],
                 rhs=x_codes[g][:, places].bitcast(FP8X4),
-                rhs_scale=x_plane[PASS_ROW * g : P, places],
+                rhs_scale=x_plane[g][PASS_ROW * g : P, places],
                 start=(g == 0),
                 stop=(g == PASSES - 1),
             )

@@ -76,19 +76,20 @@ def tile_picked_phpair_relu_p_kernel(tc, x_words, x_scales, w1, w2_words, w2_sca
         picked_scales = placed.tile([P, S], U8, name="picked_scales", align_bytes=64, offset=table_bytes - 64)
         x_plane = [keep.tile([P, S], U8, name=f"x_plane{g}", align_bytes=64) for g in range(PASSES)]
         nc.vector.tensor_copy(picked_scales[:], scale_table[:].indirect(offs_sb[:]))
-        for g in range(PASSES):
-            nc.vector.tensor_copy(x_plane[g][:].bitcast(I32), picked_scales[:].bitcast(I32))
+        nc.vector.tensor_copy(x_plane[0][:].bitcast(I32), picked_scales[:].bitcast(I32))
+        nc.gpsimd.memset(x_plane[1][:].bitcast(I32), 0)
 
-        def move_odd_rows(g):
+        def move_rows(g, odd):
             for j in range(2):
                 nc.sync.dma_start(
-                    x_plane[g][PASS_ROW * g + 2 + j : P : QUADRANT, :].bitcast(I32),
-                    x_plane[g][GROUP + PASS_ROW * g + j : P : QUADRANT, :].bitcast(I32),
+                    x_plane[g][PASS_ROW * g + 2 * odd + j : P : QUADRANT, :].bitcast(I32),
+                    x_plane[0][GROUP * odd + PASS_ROW * g + j : P : QUADRANT, :].bitcast(I32),
                 )
 
-        move_odd_rows(0)
+        move_rows(0, 1)
         load_words(last_table, 1, 0, T)
-        move_odd_rows(1)
+        for odd in range(2):
+            move_rows(1, odd)
 
         w2_plane = placed.tile([P, N], U8, name="w2_plane", align_bytes=64, offset=table_bytes)
         w2_codes = placed.tile([P, N], I32, name="w2_codes", align_bytes=64, offset=table_bytes + N)
@@ -103,7 +104,7 @@ def tile_picked_phpair_relu_p_kernel(tc, x_words, x_scales, w1, w2_words, w2_sca
         x_codes = [keep.tile([P, S], U32, name=f"x_codes{g}", align_bytes=64) for g in range(PASSES)]
         nc.vector.tensor_copy(x_codes[0][:], first_table[:].bitcast(U32).indirect(offs_sb[:]))
 
-        tags = (("a", "b"), ("c", "b"))
+        tags = (("a", "b"), ("a", "b"))
         w1_bf16 = [[keep.tile([P, 2, P, PACK], BF16, name=f"w1_bf16_{g}{d}", tag=f"w1_bf16_{tags[g][d]}", align_bytes=64) for d in range(2)] for g in range(PASSES)]
         w1_codes = [[keep.tile([P, 2 * P], U32, name=f"w1_codes{g}{d}", align_bytes=64) for d in range(2)] for g in range(PASSES)]
         w1_plane = [[keep.tile([P, 2 * P], U8, name=f"w1_plane{g}{d}", align_bytes=64) for d in range(2)] for g in range(PASSES)]
@@ -126,9 +127,9 @@ def tile_picked_phpair_relu_p_kernel(tc, x_words, x_scales, w1, w2_words, w2_sca
         for d in range(2):
             deal(0, d, 0, P, on_vector=False)
             quantize_w1(0, d)
-        deal(1, 0, 0, P, on_vector=False)
-        deal(1, 1, 0, 3 * P // 4, on_vector=True)
-        deal(1, 1, 3 * P // 4, P, on_vector=False)
+        for d in range(2):
+            deal(1, d, 0, P // 2, on_vector=True)
+            deal(1, d, P // 2, P, on_vector=False)
         for d in range(2):
             quantize_w1(1, d)
         for j0, j1 in STRETCHES:

@@ -17,6 +17,7 @@ ACT = mybir.ActivationFunctionType
 
 P = 128
 PACK = 4
+ALIGN = 256
 PASSES = K // (P * PACK)
 BANK = 512
 GROUP = 16
@@ -50,15 +51,15 @@ def tile_picked_phpair_relu_p_kernel(tc, x_words, x_scales, w1, w2_words, w2_sca
         def entries(list_sb, j0, j1):
             return list_sb[:, j0 // GROUP : j1 // GROUP]
 
-        scale_table = keep.tile([P, T], U8, name="scale_table", align_bytes=64)
+        scale_table = keep.tile([P, T], U8, name="scale_table", align_bytes=ALIGN)
         nc.gpsimd.memset(scale_table[:].bitcast(I32), 0)
 
         def load_words(table, g, c0, c1):
             nc.sync.dma_start(table[:, c0:c1], x_words[g].rearrange("p n t -> p (n t)").bitcast(I32)[:, c0:c1])
 
-        first_table = keep.tile([P, T], I32, name="first_table", align_bytes=64)
+        first_table = keep.tile([P, T], I32, name="first_table", align_bytes=ALIGN)
         w1_rows = w1.rearrange("(g p t) c -> g p t c", g=PASSES, t=PACK)
-        w1_raw = [keep.tile([P, PACK, H], F32, name=f"w1_raw{g}") for g in range(PASSES)]
+        w1_raw = [keep.tile([P, PACK, H], F32, name=f"w1_raw{g}", align_bytes=ALIGN) for g in range(PASSES)]
 
         load_words(first_table, 0, 0, FIRST_TOKENS)
         nc.sync.dma_start(offs_sb[:], offs)
@@ -72,9 +73,9 @@ def tile_picked_phpair_relu_p_kernel(tc, x_words, x_scales, w1, w2_words, w2_sca
             nc.sync.dma_start(w1_raw[g][:], w1_rows[g])
 
         table_bytes = 4 * T
-        last_table = placed.tile([P, T], I32, name="last_table", align_bytes=64, offset=0)
-        picked_scales = placed.tile([P, S], U8, name="picked_scales", align_bytes=64, offset=table_bytes - 64)
-        x_plane = [keep.tile([P, S], U8, name=f"x_plane{g}", align_bytes=64) for g in range(PASSES)]
+        last_table = placed.tile([P, T], I32, name="last_table", align_bytes=ALIGN, offset=0)
+        picked_scales = placed.tile([P, S], U8, name="picked_scales", align_bytes=ALIGN, offset=table_bytes - ALIGN)
+        x_plane = [keep.tile([P, S], U8, name=f"x_plane{g}", align_bytes=ALIGN) for g in range(PASSES)]
         nc.vector.tensor_copy(picked_scales[:], scale_table[:].indirect(offs_sb[:]))
         nc.vector.tensor_copy(x_plane[0][:].bitcast(I32), picked_scales[:].bitcast(I32))
         nc.gpsimd.memset(x_plane[1][:].bitcast(I32), 0)
@@ -91,8 +92,8 @@ def tile_picked_phpair_relu_p_kernel(tc, x_words, x_scales, w1, w2_words, w2_sca
         for odd in range(2):
             move_rows(1, odd)
 
-        w2_plane = placed.tile([P, N], U8, name="w2_plane", align_bytes=64, offset=table_bytes)
-        w2_codes = placed.tile([P, N], I32, name="w2_codes", align_bytes=64, offset=table_bytes + N)
+        w2_plane = placed.tile([P, N], U8, name="w2_plane", align_bytes=ALIGN, offset=table_bytes)
+        w2_codes = placed.tile([P, N], I32, name="w2_codes", align_bytes=ALIGN, offset=table_bytes + ALIGN)
         nc.gpsimd.memset(w2_plane[:].bitcast(I32), 0)
         nc.sync.dma_start(w2_codes[:], w2_words[0].rearrange("p n t -> p (n t)").bitcast(I32))
         for q in range(P // QUADRANT):
@@ -101,13 +102,13 @@ def tile_picked_phpair_relu_p_kernel(tc, x_words, x_scales, w1, w2_words, w2_sca
                 w2_scales[0].bitcast(I32)[4 * q : 4 * q + 4, :],
             )
 
-        x_codes = [keep.tile([P, S], U32, name=f"x_codes{g}", align_bytes=64) for g in range(PASSES)]
+        x_codes = [keep.tile([P, S], U32, name=f"x_codes{g}", align_bytes=ALIGN) for g in range(PASSES)]
         nc.vector.tensor_copy(x_codes[0][:], first_table[:].bitcast(U32).indirect(offs_sb[:]))
 
         tags = (("a", "b"), ("a", "b"))
-        w1_bf16 = [[keep.tile([P, 2, P, PACK], BF16, name=f"w1_bf16_{g}{d}", tag=f"w1_bf16_{tags[g][d]}", align_bytes=64) for d in range(2)] for g in range(PASSES)]
-        w1_codes = [[keep.tile([P, 2 * P], U32, name=f"w1_codes{g}{d}", align_bytes=64) for d in range(2)] for g in range(PASSES)]
-        w1_plane = [[keep.tile([P, 2 * P], U8, name=f"w1_plane{g}{d}", align_bytes=64) for d in range(2)] for g in range(PASSES)]
+        w1_bf16 = [[keep.tile([P, 2, P, PACK], BF16, name=f"w1_bf16_{g}{d}", tag=f"w1_bf16_{tags[g][d]}", align_bytes=ALIGN) for d in range(2)] for g in range(PASSES)]
+        w1_codes = [[keep.tile([P, 2 * P], U32, name=f"w1_codes{g}{d}", align_bytes=ALIGN) for d in range(2)] for g in range(PASSES)]
+        w1_plane = [[keep.tile([P, 2 * P], U8, name=f"w1_plane{g}{d}", align_bytes=ALIGN) for d in range(2)] for g in range(PASSES)]
 
         def deal(g, d, m0, m1, on_vector):
             dst = w1_bf16[g][d][:, :, m0:m1, :].rearrange("p e m t -> p m t e")
@@ -135,7 +136,7 @@ def tile_picked_phpair_relu_p_kernel(tc, x_words, x_scales, w1, w2_words, w2_sca
         for j0, j1 in STRETCHES:
             nc.vector.tensor_copy(x_codes[1][:, j0:j1], last_table[:].bitcast(U32).indirect(entries(offs_sb, j0, j1)))
 
-        h = [keep.tile([P, S], F32, name=f"h{s}") for s in range(PACK)]
+        h = [keep.tile([P, S], F32, name=f"h{s}", align_bytes=ALIGN) for s in range(PACK)]
         sums = [[None] * len(STRETCHES) for s in range(PACK)]
 
         def multiply(s, u, g):
@@ -160,8 +161,8 @@ def tile_picked_phpair_relu_p_kernel(tc, x_words, x_scales, w1, w2_words, w2_sca
             else:
                 nc.scalar.copy(h[s][:, places], sums[s][u][:])
 
-        h_right = [keep.tile([P, V], F32, name=f"h_right{s}", align_bytes=64) for s in range(PACK)]
-        diff = keep.tile([P, PACK, V], F32, name="diff", align_bytes=64)
+        h_right = [keep.tile([P, V], F32, name=f"h_right{s}", align_bytes=ALIGN) for s in range(PACK)]
+        diff = keep.tile([P, PACK, V], F32, name="diff", align_bytes=ALIGN)
 
         def fetch_right(s, v0, v1, on_vector):
             window = h[s][:].indirect(entries(right_sb, v0, v1))
@@ -173,7 +174,7 @@ def tile_picked_phpair_relu_p_kernel(tc, x_words, x_scales, w1, w2_words, w2_sca
         def subtract(s, v0, v1):
             nc.vector.tensor_tensor(diff[:, s, v0:v1], h[s][:].indirect(entries(left_sb, v0, v1)), h_right[s][:, v0:v1], ALU.subtract)
 
-        z_bf16 = [keep.tile([P, v1 - v0, PACK], BF16, name=f"z_bf16_{c}", align_bytes=64) for c, (v0, v1) in enumerate(PAIR_CHUNKS)]
+        z_bf16 = [keep.tile([P, v1 - v0, PACK], BF16, name=f"z_bf16_{c}", align_bytes=ALIGN) for c, (v0, v1) in enumerate(PAIR_CHUNKS)]
 
         def rectify(c, v0, v1, on_vector):
             first = PAIR_CHUNKS[c][0]
@@ -188,8 +189,8 @@ def tile_picked_phpair_relu_p_kernel(tc, x_words, x_scales, w1, w2_words, w2_sca
 
         def second_product(c, b):
             v0, v1 = PAIR_CHUNKS[c]
-            z_codes = keep.tile([P, v1 - v0], U32, name=f"z_codes{c}", align_bytes=64)
-            z_plane = keep.tile([P, v1 - v0], U8, name=f"z_plane{c}", align_bytes=64)
+            z_codes = keep.tile([P, v1 - v0], U32, name=f"z_codes{c}", align_bytes=ALIGN)
+            z_plane = keep.tile([P, v1 - v0], U8, name=f"z_plane{c}", align_bytes=ALIGN)
             nc.vector.quantize_mx(out=z_codes[:].bitcast(FP8X4), scales=z_plane[:], in_=z_bf16[c][:].rearrange("p v s -> p (v s)"))
             nc.tensor.matmul_mx(
                 out=out_sums[b][:, v0 - STORES[b][0] : v1 - STORES[b][0]],
@@ -203,7 +204,7 @@ def tile_picked_phpair_relu_p_kernel(tc, x_words, x_scales, w1, w2_words, w2_sca
 
         def store(b, tag, on_vector):
             v0, v1 = STORES[b]
-            result = keep.tile([P, v1 - v0], F32, name=f"result{b}", tag=tag, align_bytes=64)
+            result = keep.tile([P, v1 - v0], F32, name=f"result{b}", tag=tag, align_bytes=ALIGN)
             if on_vector:
                 nc.vector.tensor_copy(result[:], out_sums[b][:])
             else:

from contextlib import ExitStack

import concourse.mybir as mybir

K, T, S, H, N, V = 1024, 2048, 1024, 512, 128, 512
FLOPS = 2 * K * H * S + 2 * H * N * V

F32 = mybir.dt.float32
BF16 = mybir.dt.bfloat16
I32 = mybir.dt.int32
U32 = mybir.dt.uint32
U16 = mybir.dt.uint16
U8 = mybir.dt.uint8
FP8X4 = mybir.dt.float8_e4m3fn_x4
ALU = mybir.AluOpType
ACT = mybir.ActivationFunctionType

P = 128
PACK = 4
ALIGN = 256
PASSES = K // (P * PACK)
BANK = 512
GROUP = 16
QUADRANT = 32
LINE = 4
PASS_ROW = 8

FIRST_TOKENS = 3 * T // 8

STRETCHES = ((0, 256), (256, 768), (768, S))
BANKS = ((0, 4, 6), (1, 5, 7), (2, 0, 1), (3, 2, 3))

HALF = V // 2
PAIR_CHUNKS = ((0, 256), (256, 384), (384, 448), (448, V))
STORES = ((0, 256), (256, 448), (448, V))
FIRST_OUT_BANK = 4


def tile_picked_phpair_relu_p_kernel(tc, x_words, x_scales, w1, w2_words, w2_scales, offs, left, right, out):
    nc = tc.nc
    with ExitStack() as ctx:
        lists = ctx.enter_context(tc.tile_pool(name="lists", bufs=1))
        keep = ctx.enter_context(tc.tile_pool(name="keep", bufs=1))
        placed = ctx.enter_context(tc.tile_pool(name="placed", bufs=1))
        psum = ctx.enter_context(tc.psum_pool(name="psum", bufs=1))

        offs_sb = lists.tile([P, S // GROUP], U16, name="offs_sb")
        left_sb = lists.tile([P, V // GROUP], U16, name="left_sb")
        right_sb = lists.tile([P, V // GROUP], U16, name="right_sb")

        def entries(list_sb, j0, j1):
            return list_sb[:, j0 // GROUP : j1 // GROUP]

        scale_table = keep.tile([P, T], U8, name="scale_table", align_bytes=ALIGN)
        nc.gpsimd.memset(scale_table[:].bitcast(I32), 0)

        def load_words(table, g, c0, c1):
            nc.sync.dma_start(table[:, c0:c1], x_words[g].rearrange("p n t -> p (n t)").bitcast(I32)[:, c0:c1])

        first_table = keep.tile([P, T], I32, name="first_table", align_bytes=ALIGN)
        w1_rows = w1.rearrange("(g p t) c -> g p t c", g=PASSES, t=PACK)
        w1_raw = [keep.tile([P, PACK, H], F32, name=f"w1_raw{g}", align_bytes=ALIGN) for g in range(PASSES)]

        load_words(first_table, 0, 0, FIRST_TOKENS)
        nc.sync.dma_start(offs_sb[:], offs)
        nc.sync.dma_start(left_sb[:], left)
        nc.sync.dma_start(right_sb[:], right)
        scale_rows = x_scales.bitcast(I32).rearrange("g (r j) c -> j r g c", j=2)
        for j in range(2):
            nc.sync.dma_start(scale_table[j:P:PASS_ROW, :].bitcast(I32), scale_rows[j])
        load_words(first_table, 0, FIRST_TOKENS, T)
        for g in range(PASSES):
            nc.sync.dma_start(w1_raw[g][:], w1_rows[g])

        table_bytes = 4 * T
        last_table = placed.tile([P, T], I32, name="last_table", align_bytes=ALIGN, offset=0)
        picked_scales = placed.tile([P, S], U8, name="picked_scales", align_bytes=ALIGN, offset=table_bytes - ALIGN)
        x_plane = [keep.tile([P, S], U8, name=f"x_plane{g}", align_bytes=ALIGN) for g in range(PASSES)]
        nc.vector.tensor_copy(picked_scales[:], scale_table[:].indirect(offs_sb[:]))
        nc.vector.tensor_copy(x_plane[0][:].bitcast(I32), picked_scales[:].bitcast(I32))
        nc.gpsimd.memset(x_plane[1][:].bitcast(I32), 0)

        def move_rows(g, odd):
            for j in range(2):
                nc.sync.dma_start(
                    x_plane[g][PASS_ROW * g + 2 * odd + j : P : QUADRANT, :].bitcast(I32),
                    x_plane[0][GROUP * odd + PASS_ROW * g + j : P : QUADRANT, :].bitcast(I32),
                )

        move_rows(0, 1)
        load_words(last_table, 1, 0, T)
        for odd in range(2):
            move_rows(1, odd)

        w2_plane = placed.tile([P, N], U8, name="w2_plane", align_bytes=ALIGN, offset=table_bytes)
        w2_codes = placed.tile([P, N], I32, name="w2_codes", align_bytes=ALIGN, offset=table_bytes + ALIGN)
        nc.gpsimd.memset(w2_plane[:].bitcast(I32), 0)
        nc.sync.dma_start(w2_codes[:], w2_words[0].rearrange("p n t -> p (n t)").bitcast(I32))
        for q in range(P // QUADRANT):
            nc.sync.dma_start(
                w2_plane[QUADRANT * q : QUADRANT * q + 4, :].bitcast(I32),
                w2_scales[0].bitcast(I32)[4 * q : 4 * q + 4, :],
            )

        x_codes = [keep.tile([P, S], U32, name=f"x_codes{g}", align_bytes=ALIGN) for g in range(PASSES)]
        nc.vector.tensor_copy(x_codes[0][:], first_table[:].bitcast(U32).indirect(offs_sb[:]))

        tags = (("a", "b"), ("a", "b"))
        w1_bf16 = [[keep.tile([P, 2, P, PACK], BF16, name=f"w1_bf16_{g}{d}", tag=f"w1_bf16_{tags[g][d]}", align_bytes=ALIGN) for d in range(2)] for g in range(PASSES)]
        w1_codes = [[keep.tile([P, 2 * P], U32, name=f"w1_codes{g}{d}", align_bytes=ALIGN) for d in range(2)] for g in range(PASSES)]
        w1_plane = [[keep.tile([P, 2 * P], U8, name=f"w1_plane{g}{d}", align_bytes=ALIGN) for d in range(2)] for g in range(PASSES)]

        def deal(g, d, m0, m1, on_vector):
            dst = w1_bf16[g][d][:, :, m0:m1, :].rearrange("p e m t -> p m t e")
            src = w1_raw[g][:].rearrange("p t (m s) -> p m t s", s=PACK)[:, m0:m1, :, 2 * d : 2 * d + 2]
            if on_vector:
                nc.vector.tensor_copy(dst, src)
            else:
                nc.scalar.copy(dst, src)

        def quantize_w1(g, d):
            nc.vector.quantize_mx(
                out=w1_codes[g][d][:].bitcast(FP8X4),
                scales=w1_plane[g][d][:],
                in_=w1_bf16[g][d][:].rearrange("p e m t -> p (e m t)"),
            )

        for d in range(2):
            deal(0, d, 0, P, on_vector=False)
            quantize_w1(0, d)
        for d in range(2):
            deal(1, d, 0, P // 2, on_vector=True)
            deal(1, d, P // 2, P, on_vector=False)
        for d in range(2):
            quantize_w1(1, d)
        for j0, j1 in STRETCHES:
            nc.vector.tensor_copy(x_codes[1][:, j0:j1], last_table[:].bitcast(U32).indirect(entries(offs_sb, j0, j1)))

        h = [keep.tile([P, S], F32, name=f"h{s}", align_bytes=ALIGN) for s in range(PACK)]
        sums = [[None] * len(STRETCHES) for s in range(PACK)]

        def multiply(s, u, g):
            places = slice(*STRETCHES[u])
            if g == 0:
                sums[s][u] = psum.tile([P, places.stop - places.start], F32, name=f"sums{s}{u}", tag=f"bank{BANKS[s][u]}")
            d, columns = s // 2, slice((s % 2) * P, (s % 2 + 1) * P)
            nc.tensor.matmul_mx(
                out=sums[s][u][:],
                lhsT=w1_codes[g][d][:, columns].bitcast(FP8X4),
                lhsT_scale=w1_plane[g][d][:, columns],
                rhs=x_codes[g][:, places].bitcast(FP8X4),
                rhs_scale=x_plane[g][PASS_ROW * g : P, places],
                start=(g == 0),
                stop=(g == PASSES - 1),
            )

        def empty(s, u, on_vector):
            places = slice(*STRETCHES[u])
            if on_vector:
                nc.vector.tensor_copy(h[s][:, places], sums[s][u][:])
            else:
                nc.scalar.copy(h[s][:, places], sums[s][u][:])

        h_right = [keep.tile([P, V], F32, name=f"h_right{s}", align_bytes=ALIGN) for s in range(PACK)]
        diff = keep.tile([P, PACK, V], F32, name="diff", align_bytes=ALIGN)

        def fetch_right(s, v0, v1, on_vector):
            window = h[s][:].indirect(entries(right_sb, v0, v1))
            if on_vector:
                nc.vector.tensor_copy(h_right[s][:, v0:v1], window)
            else:
                nc.scalar.activation(h_right[s][:, v0:v1], window, ACT.Copy)

        def subtract(s, v0, v1):
            nc.vector.tensor_tensor(diff[:, s, v0:v1], h[s][:].indirect(entries(left_sb, v0, v1)), h_right[s][:, v0:v1], ALU.subtract)

        z_bf16 = [keep.tile([P, v1 - v0, PACK], BF16, name=f"z_bf16_{c}", align_bytes=ALIGN) for c, (v0, v1) in enumerate(PAIR_CHUNKS)]

        def rectify(c, v0, v1, on_vector):
            first = PAIR_CHUNKS[c][0]
            dst = z_bf16[c][:, v0 - first : v1 - first, :].rearrange("p (a b) s -> p a s b", b=LINE)
            src = diff[:, :, v0:v1].rearrange("p s (a b) -> p a s b", b=LINE)
            if on_vector:
                nc.vector.tensor_scalar(dst, src, 0.0, None, ALU.max)
            else:
                nc.scalar.activation(dst, src, ACT.Relu)

        out_sums = [psum.tile([P, v1 - v0], F32, name=f"out_sums{b}", tag=f"bank{FIRST_OUT_BANK + b}") for b, (v0, v1) in enumerate(STORES)]

        def second_product(c, b):
            v0, v1 = PAIR_CHUNKS[c]
            z_codes = keep.tile([P, v1 - v0], U32, name=f"z_codes{c}", align_bytes=ALIGN)
            z_plane = keep.tile([P, v1 - v0], U8, name=f"z_plane{c}", align_bytes=ALIGN)
            nc.vector.quantize_mx(out=z_codes[:].bitcast(FP8X4), scales=z_plane[:], in_=z_bf16[c][:].rearrange("p v s -> p (v s)"))
            nc.tensor.matmul_mx(
                out=out_sums[b][:, v0 - STORES[b][0] : v1 - STORES[b][0]],
                lhsT=w2_codes[:].bitcast(FP8X4),
                lhsT_scale=w2_plane[:],
                rhs=z_codes[:].bitcast(FP8X4),
                rhs_scale=z_plane[:],
                start=True,
                stop=True,
            )

        def store(b, tag, on_vector):
            v0, v1 = STORES[b]
            result = keep.tile([P, v1 - v0], F32, name=f"result{b}", tag=tag, align_bytes=ALIGN)
            if on_vector:
                nc.vector.tensor_copy(result[:], out_sums[b][:])
            else:
                nc.scalar.copy(result[:], out_sums[b][:])
            nc.sync.dma_start(out[:, v0:v1], result[:])

        for s in range(PACK):
            multiply(s, 0, 0)
        for s in range(2):
            for u in (1, 2):
                multiply(s, u, 0)
        for s in range(PACK):
            multiply(s, 0, 1)
            empty(s, 0, on_vector=(s == 3))
        for u in (1, 2):
            for s in range(2):
                multiply(s, u, 1)
                empty(s, u, on_vector=(s, u) == (1, 1))
        for s in range(2, PACK):
            for u in (1, 2):
                for g in range(PASSES):
                    multiply(s, u, g)
        empty(2, 1, on_vector=False)
        fetch_right(1, 0, V, on_vector=False)
        empty(2, 2, on_vector=False)
        for u in (1, 2):
            empty(3, u, on_vector=False)
        for v0 in (0, HALF):
            for s in (2, 3):
                fetch_right(s, v0, v0 + HALF, on_vector=False)
        for v0 in (0, HALF):
            fetch_right(0, v0, v0 + HALF, on_vector=True)
        for v0 in (0, HALF):
            subtract(0, v0, v0 + HALF)
        subtract(1, 0, V)
        subtract(2, 0, HALF)
        subtract(3, 0, HALF)
        rectify(0, 0, 192, on_vector=False)
        subtract(2, HALF, V)
        subtract(3, 256, 384)
        rectify(1, 256, 384, on_vector=False)
        rectify(0, 192, 256, on_vector=True)
        subtract(3, 384, 448)
        rectify(2, 384, 448, on_vector=False)
        second_product(0, 0)
        subtract(3, 448, V)
        rectify(3, 448, V, on_vector=False)
        second_product(1, 1)
        second_product(2, 1)
        second_product(3, 2)
        store(0, "result0", on_vector=False)
        store(1, "result1", on_vector=False)
        store(2, "result2", on_vector=True)
